import numpy as np
import ml_dtypes


def mxq(x, axis, fmt="e4m3"):
    dtype, down = {"e4m3": (ml_dtypes.float8_e4m3fn, 7), "e5m2": (ml_dtypes.float8_e5m2, 14)}[fmt]
    v = np.moveaxis(np.asarray(x, np.float32).astype(ml_dtypes.bfloat16).astype(np.float64), axis, -1)
    blocks = v.reshape(v.shape[:-1] + (-1, 32))
    amax = np.abs(blocks).max(-1, keepdims=True)
    byte = np.maximum(np.where(amax > 0, np.frexp(amax)[1] - 1 + 127, 0) - down, 1)
    scale = np.exp2(byte - 127.0)
    codes = (blocks / scale).astype(np.float32).astype(dtype).astype(np.float64)
    return np.moveaxis((codes * scale).reshape(v.shape), -1, axis)


WIDE = False


def mx_kscale(k):
    if not WIDE:
        return np.ones(k)
    levels = np.array([10, -10, 5, -5, 0])
    if k % 512:
        return np.exp2(np.random.permutation(np.resize(levels, k // 32))).repeat(32)
    a = np.empty((k // 512, 16))
    for p in range(k // 512):
        a[p, :8] = np.random.permutation(np.resize(levels, 8))
        for g in range(8):
            far = levels[np.abs(levels - a[p, g]) >= 10]
            a[p, g + 8] = far[np.random.randint(len(far))]
    return np.exp2(a.ravel()).repeat(32)


def f64(x):
    return np.asarray(x).astype(np.float64)


def striped(idx):
    return np.tile(idx.reshape(-1, 16).T, (8, 1)).astype(np.uint16)


def unstriped(offs):
    return offs[:16].T.reshape(-1).astype(np.int64)


def striped8(idx):
    return np.concatenate([x.reshape(-1, 16).T for x in idx]).astype(np.uint16)


def runs(offs, k):
    lists = np.stack([offs[16 * r : 16 * r + 16].T.reshape(-1) for r in range(8)]).astype(np.int64)
    return lists[np.arange(k) % 512 // 64]


def pack_weight(w):
    k, n = w.shape
    w = f64(np.asarray(w, np.float32).astype(ml_dtypes.bfloat16)).reshape(k // 32, 32, n)
    amax = np.abs(w).max(1)
    byte = np.clip(np.where(amax > 0, np.frexp(amax)[1] - 1 + 127 - 7, 1), 1, 254)
    scaled = (w * np.exp2(127.0 - byte)[:, None, :]).reshape(k, n).astype(np.float32)
    words = np.ascontiguousarray(scaled.reshape(k // 512, 128, 4, n).transpose(0, 1, 3, 2)).astype(ml_dtypes.float8_e4m3fn).view(np.uint8)
    return words, np.ascontiguousarray(byte.astype(np.uint8).reshape(k // 512, 16, n))


def unpack_weight(words, scales):
    g, p, n, _ = words.shape
    vals = np.ascontiguousarray(words).view(ml_dtypes.float8_e4m3fn).astype(np.float64) * np.repeat(np.exp2(scales.astype(np.float64) - 127.0), 8, axis=1)[..., None]
    return vals.transpose(0, 1, 3, 2).reshape(g * 512, n)


K, T, S, N, H = 512, 2048, 512, 512, 512


def setup_inputs():
    n = np.random.standard_normal
    s = mx_kscale(K)[:, None]
    u = mx_kscale(H)
    packed_xT = pack_weight(n((K, T)) * s)
    return {
        "x_words": packed_xT[0],
        "x_scales": packed_xT[1],
        "w1": (n((K, H)) / np.sqrt(K) / s * u).astype(np.float32),
        "w2": (n((H, N)) / np.sqrt(H) / u[:, None]).astype(np.float32),
        "offs": striped(np.random.permutation(T)[:S]),
        "par": striped8(np.random.randint(0, S, (8, S))),
    }


def reference(x_words, x_scales, w1, w2, offs, par):
    xq = unpack_weight(x_words, x_scales)[:, unstriped(offs)]
    y = mxq(f64(w1), 0, "e4m3").T @ xq
    p = y[np.arange(H)[:, None], runs(par, H)]
    q = p[np.arange(H)[:, None], runs(par, H)]
    z = y + p - q
    return mxq(f64(w2), 0, "e4m3").T @ mxq(z, 0, "e4m3")

@@ -1,0 +1,138 @@
+from contextlib import ExitStack
+
+import concourse.mybir as mybir
+
+K, T, S, H, N = 512, 2048, 512, 512, 512
+FLOPS = 2 * K * H * S + 2 * H * N * S
+
+F32 = mybir.dt.float32
+BF16 = mybir.dt.bfloat16
+I32 = mybir.dt.int32
+U32 = mybir.dt.uint32
+U16 = mybir.dt.uint16
+U8 = mybir.dt.uint8
+FP8X4 = mybir.dt.float8_e4m3fn_x4
+COPY = mybir.ActivationFunctionType.Copy
+ADD = mybir.AluOpType.add
+
+P = 128
+PACK = 4
+HALF = S // 2
+PIECES = ((0, 256), (256, 128), (384, 128))
+W1_VECTOR_COLS = 40
+
+
+def tile_picked_ptrjump_none_p_kernel(tc, x_words, x_scales, w1, w2, offs, par, out):
+    nc = tc.nc
+    with ExitStack() as ctx:
+        keep = ctx.enter_context(tc.tile_pool(name="keep", bufs=1))
+        psum = ctx.enter_context(tc.psum_pool(name="psum", bufs=1))
+
+        offs_t = keep.tile([P, S // 16], U16, name="offs_t")
+        par_t = keep.tile([P, S // 16], U16, name="par_t")
+        words = keep.tile([P, T], U32, name="words", align_bytes=64)
+        scale_rows = keep.tile([P, T], U8, name="scale_rows", align_bytes=64)
+        w1_raw = [keep.tile([P, PACK, H // 2], F32, name="w1_raw%d" % h) for h in range(2)]
+        w2_raw = keep.tile([P, PACK, N], F32, name="w2_raw")
+
+        nc.vector.memset(scale_rows[:].bitcast(I32), 0)
+        nc.sync.dma_start(words[:].bitcast(I32), x_words[0].rearrange("p n r -> p (n r)").bitcast(I32))
+        nc.sync.dma_start(offs_t[:], offs)
+        for q in range(4):
+            nc.scalar.dma_start(scale_rows[32 * q : 32 * q + 4, :].bitcast(I32), x_scales[0, 4 * q : 4 * q + 4, :].bitcast(I32))
+        w1_rows = w1.rearrange("(p j) c -> p j c", j=PACK)
+        for h in range(2):
+            nc.sync.dma_start(w1_raw[h][:], w1_rows[:, :, h * (H // 2) : (h + 1) * (H // 2)])
+        nc.sync.dma_start(par_t[:], par)
+        nc.sync.dma_start(w2_raw[:], w2.rearrange("(p j) c -> p j c", j=PACK))
+
+        x_codes = keep.tile([P, S], U32, name="x_codes", align_bytes=64)
+        x_sc = keep.tile([P, S], U8, name="x_sc", align_bytes=64)
+        nc.vector.tensor_copy(x_sc[:], scale_rows[:].indirect(offs_t[:]))
+        nc.vector.tensor_copy(x_codes[:], words[:].indirect(offs_t[:]))
+
+        w1_codes = [keep.tile([P, P], U32, name="w1_codes%d" % t, tag="w1_codes%d" % t, align_bytes=64) for t in range(PACK)]
+        w1_sc = [keep.tile([P, P], U8, name="w1_sc%d" % t, align_bytes=64) for t in range(PACK)]
+        for h in range(2):
+            w1_bf = keep.tile([P, PACK, P // 2, PACK], BF16, name="w1_bf%d" % h, align_bytes=64)
+            src = w1_raw[h][:].rearrange("p j (m t) -> p m j t", t=PACK)
+            dst = w1_bf[:].rearrange("p t m j -> p m j t")
+            nc.vector.tensor_copy(dst[:, :W1_VECTOR_COLS], src[:, :W1_VECTOR_COLS])
+            nc.scalar.copy(dst[:, W1_VECTOR_COLS:], src[:, W1_VECTOR_COLS:])
+            for t in range(PACK):
+                cols = slice(h * (P // 2), (h + 1) * (P // 2))
+                nc.vector.quantize_mx(
+                    out=w1_codes[t][:, cols].bitcast(FP8X4),
+                    scales=w1_sc[t][:, cols],
+                    in_=w1_bf[:, t].rearrange("p m j -> p (m j)"),
+                )
+
+        y_neg = [keep.tile([P, S], F32, name="y_neg%d" % t) for t in range(PACK)]
+        y_pos = [keep.tile([P, S], F32, name="y_pos%d" % t) for t in range(PACK)]
+        diff = [keep.tile([P, S], F32, name="diff%d" % t) for t in range(PACK)]
+        for t in range(PACK):
+            spans = [slice(0, HALF), slice(HALF, S)] if t == 0 else [slice(0, S)]
+            banks = []
+            for b, span in enumerate(spans):
+                bank = psum.tile([P, span.stop - span.start], F32, name="y_bank%d_%d" % (t, b))
+                nc.tensor.matmul_mx(
+                    out=bank[:], lhsT=w1_codes[t][:].bitcast(FP8X4), lhsT_scale=w1_sc[t][:],
+                    rhs=x_codes[:, span].bitcast(FP8X4), rhs_scale=x_sc[:, span], start=True, stop=True,
+                )
+                banks.append(bank)
+            if t == 0:
+                nc.scalar.activation(y_neg[t][:, spans[0]], banks[0][:], COPY, scale=-1.0)
+                nc.vector.tensor_copy(y_pos[t][:, spans[1]], banks[1][:])
+                nc.scalar.activation(y_neg[t][:, spans[1]], banks[1][:], COPY, scale=-1.0)
+                nc.vector.tensor_copy(y_pos[t][:, spans[0]], banks[0][:])
+            else:
+                nc.scalar.activation(y_neg[t][:], banks[0][:], COPY, scale=-1.0)
+                nc.scalar.copy(y_pos[t][:], banks[0][:])
+            for a in (0, HALF):
+                nc.vector.tensor_tensor(
+                    diff[t][:, a : a + HALF], y_neg[t][:].indirect(par_t[:, a // 16 : (a + HALF) // 16]),
+                    y_pos[t][:, a : a + HALF], ADD,
+                )
+
+        w2_bf = keep.tile([P, N, PACK], BF16, name="w2_bf", tag="w1_codes3", align_bytes=64)
+        nc.scalar.copy(
+            w2_bf[:].rearrange("p (c i) j -> p c j i", i=4), w2_raw[:].rearrange("p j (c i) -> p c j i", i=4)
+        )
+        w2_codes = keep.tile([P, N], U32, name="w2_codes", align_bytes=64)
+        w2_sc = keep.tile([P, N], U8, name="w2_sc", align_bytes=64)
+        nc.vector.quantize_mx(out=w2_codes[:].bitcast(FP8X4), scales=w2_sc[:], in_=w2_bf[:].rearrange("p c j -> p (c j)"))
+
+        out_rows = out.rearrange("(u p) n -> p u n", p=P)
+        for g, (a, n) in enumerate(PIECES):
+            last = g == len(PIECES) - 1
+            z = keep.tile([P, PACK, n], F32, name="z%d" % g, tag="z_bf0" if last else "z%d" % g, align_bytes=64)
+            for t in range(PACK):
+                nc.vector.tensor_tensor(
+                    z[:, t, :], diff[t][:].indirect(par_t[:, a // 16 : (a + n) // 16]), y_pos[t][:, a : a + n], ADD
+                )
+            z_bf = keep.tile([P, n, PACK], BF16, name="z_bf%d" % g, tag="z_bf%d" % g, align_bytes=64)
+            dst = z_bf[:].rearrange("p (c i) t -> p c t i", i=4)
+            src = z[:].rearrange("p t (c i) -> p c t i", i=4)
+            if last:
+                nc.vector.tensor_copy(dst, src)
+            else:
+                nc.scalar.copy(dst, src)
+            z_codes = keep.tile([P, n], U32, name="z_codes%d" % g, align_bytes=64)
+            z_sc = keep.tile([P, n], U8, name="z_sc%d" % g, align_bytes=64)
+            nc.vector.quantize_mx(out=z_codes[:].bitcast(FP8X4), scales=z_sc[:], in_=z_bf[:].rearrange("p c t -> p (c t)"))
+            for pair in range(2):
+                bank = psum.tile([P, 2, n], F32, name="o_bank%d" % pair, tag="o_bank%d" % pair)
+                for v in range(2):
+                    u = 2 * pair + v
+                    nc.tensor.matmul_mx(
+                        out=bank[:, v, :], lhsT=w2_codes[:, u * P : (u + 1) * P].bitcast(FP8X4),
+                        lhsT_scale=w2_sc[:, u * P : (u + 1) * P],
+                        rhs=z_codes[:].bitcast(FP8X4), rhs_scale=z_sc[:], start=True, stop=True,
+                    )
+                res = keep.tile([P, 2, n], F32, name="res%d_%d" % (g, pair))
+                if last and pair == 1:
+                    nc.vector.tensor_copy(res[:], bank[:])
+                else:
+                    nc.scalar.copy(res[:], bank[:])
+                queue = nc.scalar if last and pair == 0 else nc.sync
+                queue.dma_start(out_rows[:, 2 * pair : 2 * pair + 2, a : a + n], res[:])

@@ -19,7 +19,7 @@ P = 128
 PACK = 4
 HALF = S // 2
 PIECES = ((0, 256), (256, 128), (384, 128))
-W1_VECTOR_COLS = 40
+X_FIRST = 1024
 
 
 def tile_picked_ptrjump_none_p_kernel(tc, x_words, x_scales, w1, w2, offs, par, out):
@@ -30,51 +30,60 @@ def tile_picked_ptrjump_none_p_kernel(tc, x_words, x_scales, w1, w2, offs, par, 
 
         offs_t = keep.tile([P, S // 16], U16, name="offs_t")
         par_t = keep.tile([P, S // 16], U16, name="par_t")
-        words = keep.tile([P, T], U32, name="words", align_bytes=64)
+        words = keep.tile([P, T], U32, name="words", tag="words", align_bytes=64)
         scale_rows = keep.tile([P, T], U8, name="scale_rows", align_bytes=64)
-        w1_raw = [keep.tile([P, PACK, H // 2], F32, name="w1_raw%d" % h) for h in range(2)]
-        w2_raw = keep.tile([P, PACK, N], F32, name="w2_raw")
+        w1_raw = [keep.tile([P, PACK // 2, H], F32, name="w1_raw%d" % h) for h in range(2)]
 
         nc.vector.memset(scale_rows[:].bitcast(I32), 0)
-        nc.sync.dma_start(words[:].bitcast(I32), x_words[0].rearrange("p n r -> p (n r)").bitcast(I32))
+        x_rows = x_words[0].rearrange("p n r -> p (n r)").bitcast(I32)
         nc.sync.dma_start(offs_t[:], offs)
-        for q in range(4):
-            nc.scalar.dma_start(scale_rows[32 * q : 32 * q + 4, :].bitcast(I32), x_scales[0, 4 * q : 4 * q + 4, :].bitcast(I32))
+        nc.scalar.dma_start(words[:, :X_FIRST].bitcast(I32), x_rows[:, :X_FIRST])
+        nc.sync.dma_start(par_t[:], par)
+        nc.sync.dma_start(scale_rows[0:P:8, :].bitcast(I32), x_scales[0].bitcast(I32))
+        nc.sync.dma_start(words[:, X_FIRST:].bitcast(I32), x_rows[:, X_FIRST:])
         w1_rows = w1.rearrange("(p j) c -> p j c", j=PACK)
         for h in range(2):
-            nc.sync.dma_start(w1_raw[h][:], w1_rows[:, :, h * (H // 2) : (h + 1) * (H // 2)])
-        nc.sync.dma_start(par_t[:], par)
-        nc.sync.dma_start(w2_raw[:], w2.rearrange("(p j) c -> p j c", j=PACK))
+            nc.sync.dma_start(w1_raw[h][:], w1_rows[:, 2 * h : 2 * h + 2, :])
 
         x_codes = keep.tile([P, S], U32, name="x_codes", align_bytes=64)
         x_sc = keep.tile([P, S], U8, name="x_sc", align_bytes=64)
-        nc.vector.tensor_copy(x_sc[:], scale_rows[:].indirect(offs_t[:]))
+        picked_rows = keep.tile([P, S], U8, name="picked_rows", align_bytes=64)
+        nc.vector.memset(x_sc[:].bitcast(I32), 0)
+        nc.vector.tensor_copy(picked_rows[:], scale_rows[:].indirect(offs_t[:]))
+        for r in range(4):
+            nc.sync.dma_start(x_sc[r:P:32, :].bitcast(I32), picked_rows[8 * r : P : 32, :].bitcast(I32))
         nc.vector.tensor_copy(x_codes[:], words[:].indirect(offs_t[:]))
+        w2_raw = keep.tile([P, PACK, N], F32, name="w2_raw", tag="words", align_bytes=64)
+        w2_rows = w2.rearrange("(b t r) c -> t b r c", t=PACK, r=8)
+        for t in range(PACK):
+            nc.sync.dma_start(w2_raw[:, t, :], w2_rows[t])
 
         w1_codes = [keep.tile([P, P], U32, name="w1_codes%d" % t, tag="w1_codes%d" % t, align_bytes=64) for t in range(PACK)]
         w1_sc = [keep.tile([P, P], U8, name="w1_sc%d" % t, align_bytes=64) for t in range(PACK)]
+        w1_bf = [keep.tile([P, P, PACK], BF16, name="w1_bf%d" % t, align_bytes=64) for t in range(PACK)]
         for h in range(2):
-            w1_bf = keep.tile([P, PACK, P // 2, PACK], BF16, name="w1_bf%d" % h, align_bytes=64)
-            src = w1_raw[h][:].rearrange("p j (m t) -> p m j t", t=PACK)
-            dst = w1_bf[:].rearrange("p t m j -> p m j t")
-            nc.vector.tensor_copy(dst[:, :W1_VECTOR_COLS], src[:, :W1_VECTOR_COLS])
-            nc.scalar.copy(dst[:, W1_VECTOR_COLS:], src[:, W1_VECTOR_COLS:])
+            src = w1_raw[h][:].rearrange("p j (b t r) -> p t b r j", t=PACK, r=8)
             for t in range(PACK):
-                cols = slice(h * (P // 2), (h + 1) * (P // 2))
-                nc.vector.quantize_mx(
-                    out=w1_codes[t][:, cols].bitcast(FP8X4),
-                    scales=w1_sc[t][:, cols],
-                    in_=w1_bf[:, t].rearrange("p m j -> p (m j)"),
-                )
+                dst = w1_bf[t][:, :, 2 * h : 2 * h + 2].rearrange("p (b r) j -> p b r j", r=8)
+                if t < 2:
+                    nc.vector.tensor_copy(dst, src[:, t])
+                else:
+                    nc.scalar.activation(dst, src[:, t], COPY)
+        for t in range(PACK):
+            nc.vector.quantize_mx(
+                out=w1_codes[t][:].bitcast(FP8X4), scales=w1_sc[t][:], in_=w1_bf[t][:].rearrange("p m j -> p (m j)")
+            )
 
-        y_neg = [keep.tile([P, S], F32, name="y_neg%d" % t) for t in range(PACK)]
-        y_pos = [keep.tile([P, S], F32, name="y_pos%d" % t) for t in range(PACK)]
+        window = [keep.tile([P, 2 * S if t == 1 else S], F32, name="window%d" % t, tag="window%d" % t, align_bytes=64) for t in range(PACK)]
+        y_own = [keep.tile([P, S], F32, name="y_own%d" % t) for t in (1, 2, 3)]
+        y_neg = [window[t][:, :S] for t in range(PACK)]
+        y_pos = [window[1][:, S:]] + [y[:] for y in y_own]
         diff = [keep.tile([P, S], F32, name="diff%d" % t) for t in range(PACK)]
         for t in range(PACK):
             spans = [slice(0, HALF), slice(HALF, S)] if t == 0 else [slice(0, S)]
             banks = []
             for b, span in enumerate(spans):
-                bank = psum.tile([P, span.stop - span.start], F32, name="y_bank%d_%d" % (t, b))
+                bank = psum.tile([P, span.stop - span.start], F32, name="y_bank%d_%d" % (t, b), tag="bank%d" % (t + b + min(t, 1)))
                 nc.tensor.matmul_mx(
                     out=bank[:], lhsT=w1_codes[t][:].bitcast(FP8X4), lhsT_scale=w1_sc[t][:],
                     rhs=x_codes[:, span].bitcast(FP8X4), rhs_scale=x_sc[:, span], start=True, stop=True,
@@ -82,16 +91,16 @@ def tile_picked_ptrjump_none_p_kernel(tc, x_words, x_scales, w1, w2, offs, par, 
                 banks.append(bank)
             if t == 0:
                 nc.scalar.activation(y_neg[t][:, spans[0]], banks[0][:], COPY, scale=-1.0)
-                nc.vector.tensor_copy(y_pos[t][:, spans[1]], banks[1][:])
-                nc.scalar.activation(y_neg[t][:, spans[1]], banks[1][:], COPY, scale=-1.0)
-                nc.vector.tensor_copy(y_pos[t][:, spans[0]], banks[0][:])
+                nc.vector.tensor_scalar_mul(y_neg[t][:, spans[1]], banks[1][:], -1.0)
+                nc.scalar.copy(y_pos[t][:, spans[0]], banks[0][:])
+                nc.scalar.copy(y_pos[t][:, spans[1]], banks[1][:])
             else:
-                nc.scalar.activation(y_neg[t][:], banks[0][:], COPY, scale=-1.0)
-                nc.scalar.copy(y_pos[t][:], banks[0][:])
-            for a in (0, HALF):
+                nc.scalar.activation(y_neg[t], banks[0][:], COPY, scale=-1.0)
+                nc.scalar.copy(y_pos[t], banks[0][:])
+            for span in [slice(0, S)] if t == 1 else [slice(0, HALF), slice(HALF, S)]:
                 nc.vector.tensor_tensor(
-                    diff[t][:, a : a + HALF], y_neg[t][:].indirect(par_t[:, a // 16 : (a + HALF) // 16]),
-                    y_pos[t][:, a : a + HALF], ADD,
+                    diff[t][:, span], window[t][:].indirect(par_t[:, span.start // 16 : span.stop // 16]),
+                    y_pos[t][:, span], ADD,
                 )
 
         w2_bf = keep.tile([P, N, PACK], BF16, name="w2_bf", tag="w1_codes3", align_bytes=64)
@@ -105,7 +114,7 @@ def tile_picked_ptrjump_none_p_kernel(tc, x_words, x_scales, w1, w2, offs, par, 
         out_rows = out.rearrange("(u p) n -> p u n", p=P)
         for g, (a, n) in enumerate(PIECES):
             last = g == len(PIECES) - 1
-            z = keep.tile([P, PACK, n], F32, name="z%d" % g, tag="z_bf0" if last else "z%d" % g, align_bytes=64)
+            z = keep.tile([P, PACK, n], F32, name="z%d" % g, tag=("window2", "window3", "z_bf0")[g], align_bytes=64)
             for t in range(PACK):
                 nc.vector.tensor_tensor(
                     z[:, t, :], diff[t][:].indirect(par_t[:, a // 16 : (a + n) // 16]), y_pos[t][:, a : a + n], ADD
@@ -121,7 +130,7 @@ def tile_picked_ptrjump_none_p_kernel(tc, x_words, x_scales, w1, w2, offs, par, 
             z_sc = keep.tile([P, n], U8, name="z_sc%d" % g, align_bytes=64)
             nc.vector.quantize_mx(out=z_codes[:].bitcast(FP8X4), scales=z_sc[:], in_=z_bf[:].rearrange("p c t -> p (c t)"))
             for pair in range(2):
-                bank = psum.tile([P, 2, n], F32, name="o_bank%d" % pair, tag="o_bank%d" % pair)
+                bank = psum.tile([P, 2, n], F32, name="o_bank%d_%d" % (g, pair), tag="bank%d" % ((5 + 2 * g + pair) % 8))
                 for v in range(2):
                     u = 2 * pair + v
                     nc.tensor.matmul_mx(

@@ -14,11 +14,12 @@ U8 = mybir.dt.uint8
 FP8X4 = mybir.dt.float8_e4m3fn_x4
 COPY = mybir.ActivationFunctionType.Copy
 ADD = mybir.AluOpType.add
+SUB = mybir.AluOpType.subtract
 
 P = 128
 PACK = 4
 HALF = S // 2
-PIECES = ((0, 256), (256, 128), (384, 128))
+PIECES = 4
 X_FIRST = 1024
 
 
@@ -74,13 +75,17 @@ def tile_picked_ptrjump_none_p_kernel(tc, x_words, x_scales, w1, w2, offs, par, 
                 out=w1_codes[t][:].bitcast(FP8X4), scales=w1_sc[t][:], in_=w1_bf[t][:].rearrange("p m j -> p (m j)")
             )
 
-        window = [keep.tile([P, 2 * S if t == 1 else S], F32, name="window%d" % t, tag="window%d" % t, align_bytes=64) for t in range(PACK)]
-        y_own = [keep.tile([P, S], F32, name="y_own%d" % t) for t in (1, 2, 3)]
+        window = [
+            keep.tile([P, 2 * S if t in (1, 2) else S], F32, name="window%d" % t, align_bytes=64) for t in range(PACK)
+        ]
+        y_last = [keep.tile([P, HALF], F32, name="y_last%d" % b, tag="ring%d" % b, align_bytes=64) for b in range(2)]
+        y2 = keep.tile([P, S], F32, name="y2")
+        halves = [slice(0, HALF), slice(HALF, S)]
         y_neg = [window[t][:, :S] for t in range(PACK)]
-        y_pos = [window[1][:, S:]] + [y[:] for y in y_own]
+        y_pos = [window[1][:, S:], window[2][:, S:], y2[:]]
         diff = [keep.tile([P, S], F32, name="diff%d" % t) for t in range(PACK)]
         for t in range(PACK):
-            spans = [slice(0, HALF), slice(HALF, S)] if t == 0 else [slice(0, S)]
+            spans = halves if t == 0 else [slice(0, S)]
             banks = []
             for b, span in enumerate(spans):
                 bank = psum.tile([P, span.stop - span.start], F32, name="y_bank%d_%d" % (t, b), tag="bank%d" % (t + b + min(t, 1)))
@@ -93,14 +98,18 @@ def tile_picked_ptrjump_none_p_kernel(tc, x_words, x_scales, w1, w2, offs, par, 
                 nc.scalar.activation(y_neg[t][:, spans[0]], banks[0][:], COPY, scale=-1.0)
                 nc.vector.tensor_scalar_mul(y_neg[t][:, spans[1]], banks[1][:], -1.0)
                 nc.scalar.copy(y_pos[t][:, spans[0]], banks[0][:])
-                nc.scalar.copy(y_pos[t][:, spans[1]], banks[1][:])
+                nc.vector.tensor_copy(y_pos[t][:, spans[1]], banks[1][:])
             else:
                 nc.scalar.activation(y_neg[t], banks[0][:], COPY, scale=-1.0)
-                nc.scalar.copy(y_pos[t], banks[0][:])
-            for span in [slice(0, S)] if t == 1 else [slice(0, HALF), slice(HALF, S)]:
+                if t < 3:
+                    nc.scalar.copy(y_pos[t], banks[0][:])
+                else:
+                    for b in range(2):
+                        nc.scalar.copy(y_last[b][:], banks[0][:, halves[b]])
+            for b, span in enumerate([slice(0, S)] if t in (1, 2) else halves):
                 nc.vector.tensor_tensor(
                     diff[t][:, span], window[t][:].indirect(par_t[:, span.start // 16 : span.stop // 16]),
-                    y_pos[t][:, span], ADD,
+                    y_pos[t][:, span] if t < 3 else y_last[b][:], ADD,
                 )
 
         w2_bf = keep.tile([P, N, PACK], BF16, name="w2_bf", tag="w1_codes3", align_bytes=64)
@@ -109,39 +118,69 @@ def tile_picked_ptrjump_none_p_kernel(tc, x_words, x_scales, w1, w2, offs, par, 
         )
         w2_codes = keep.tile([P, N], U32, name="w2_codes", align_bytes=64)
         w2_sc = keep.tile([P, N], U8, name="w2_sc", align_bytes=64)
-        nc.vector.quantize_mx(out=w2_codes[:].bitcast(FP8X4), scales=w2_sc[:], in_=w2_bf[:].rearrange("p c j -> p (c j)"))
 
         out_rows = out.rearrange("(u p) n -> p u n", p=P)
-        for g, (a, n) in enumerate(PIECES):
-            last = g == len(PIECES) - 1
-            z = keep.tile([P, PACK, n], F32, name="z%d" % g, tag=("window2", "window3", "z_bf0")[g], align_bytes=64)
+        z_bf = [keep.tile([P, P, PACK], BF16, name="z_bf%d" % g, align_bytes=64) for g in range(PIECES)]
+        z_codes = [keep.tile([P, P], U32, name="z_codes%d" % g, align_bytes=64) for g in range(PIECES)]
+        z_sc = [keep.tile([P, P], U8, name="z_sc%d" % g, align_bytes=64) for g in range(PIECES)]
+
+        def second_hop(g):
+            z = keep.tile([P, PACK, P], F32, name="z%d" % g, tag="ring%d" % (g % 2), align_bytes=64)
             for t in range(PACK):
                 nc.vector.tensor_tensor(
-                    z[:, t, :], diff[t][:].indirect(par_t[:, a // 16 : (a + n) // 16]), y_pos[t][:, a : a + n], ADD
+                    z[:, t, :], diff[t][:].indirect(par_t[:, g * 8 : (g + 1) * 8]), y_neg[t][:, g * P : (g + 1) * P], SUB
                 )
-            z_bf = keep.tile([P, n, PACK], BF16, name="z_bf%d" % g, tag="z_bf%d" % g, align_bytes=64)
-            dst = z_bf[:].rearrange("p (c i) t -> p c t i", i=4)
-            src = z[:].rearrange("p t (c i) -> p c t i", i=4)
-            if last:
-                nc.vector.tensor_copy(dst, src)
-            else:
-                nc.scalar.copy(dst, src)
-            z_codes = keep.tile([P, n], U32, name="z_codes%d" % g, align_bytes=64)
-            z_sc = keep.tile([P, n], U8, name="z_sc%d" % g, align_bytes=64)
-            nc.vector.quantize_mx(out=z_codes[:].bitcast(FP8X4), scales=z_sc[:], in_=z_bf[:].rearrange("p c t -> p (c t)"))
-            for pair in range(2):
-                bank = psum.tile([P, 2, n], F32, name="o_bank%d_%d" % (g, pair), tag="bank%d" % ((5 + 2 * g + pair) % 8))
-                for v in range(2):
-                    u = 2 * pair + v
-                    nc.tensor.matmul_mx(
-                        out=bank[:, v, :], lhsT=w2_codes[:, u * P : (u + 1) * P].bitcast(FP8X4),
-                        lhsT_scale=w2_sc[:, u * P : (u + 1) * P],
-                        rhs=z_codes[:].bitcast(FP8X4), rhs_scale=z_sc[:], start=True, stop=True,
-                    )
-                res = keep.tile([P, 2, n], F32, name="res%d_%d" % (g, pair))
-                if last and pair == 1:
-                    nc.vector.tensor_copy(res[:], bank[:])
-                else:
-                    nc.scalar.copy(res[:], bank[:])
-                queue = nc.scalar if last and pair == 0 else nc.sync
-                queue.dma_start(out_rows[:, 2 * pair : 2 * pair + 2, a : a + n], res[:])
+            return z
+
+        def weave(engine_copy, g, z, lo, hi):
+            engine_copy(
+                z_bf[g][:, :, lo:hi].rearrange("p (c i) t -> p c t i", i=4),
+                z[:, lo:hi, :].rearrange("p t (c i) -> p c t i", i=4),
+            )
+
+        def quantize(g):
+            nc.vector.quantize_mx(
+                out=z_codes[g][:].bitcast(FP8X4), scales=z_sc[g][:], in_=z_bf[g][:].rearrange("p c t -> p (c t)")
+            )
+
+        def product(g, u0, rows, bank_no):
+            bank = psum.tile([P, rows, P], F32, name="o_bank%d_%d" % (g, u0), tag="bank%d" % bank_no)
+            for v in range(rows):
+                u = u0 + v
+                nc.tensor.matmul_mx(
+                    out=bank[:, v, :], lhsT=w2_codes[:, u * P : (u + 1) * P].bitcast(FP8X4),
+                    lhsT_scale=w2_sc[:, u * P : (u + 1) * P],
+                    rhs=z_codes[g][:].bitcast(FP8X4), rhs_scale=z_sc[g][:], start=True, stop=True,
+                )
+            return bank
+
+        def leave(engine_copy, queue, g, u0, rows, bank):
+            res = keep.tile([P, rows, P], F32, name="res%d_%d" % (g, u0))
+            engine_copy(res[:], bank[:])
+            queue.dma_start(out_rows[:, u0 : u0 + rows, g * P : (g + 1) * P], res[:])
+
+        on_scalar, on_vector = nc.scalar.copy, nc.vector.tensor_copy
+        z = second_hop(0)
+        weave(on_scalar, 0, z, 0, 4)
+        z = second_hop(1)
+        weave(on_scalar, 1, z, 0, 4)
+        nc.vector.quantize_mx(out=w2_codes[:].bitcast(FP8X4), scales=w2_sc[:], in_=w2_bf[:].rearrange("p c j -> p (c j)"))
+        quantize(0)
+        bank = product(0, 0, 4, 5)
+        leave(on_scalar, nc.sync, 0, 0, 4, bank)
+        z = second_hop(2)
+        weave(on_scalar, 2, z, 0, 4)
+        quantize(1)
+        bank = product(1, 0, 4, 6)
+        z = second_hop(3)
+        weave(on_scalar, 3, z, 0, 2)
+        leave(on_scalar, nc.sync, 1, 0, 4, bank)
+        quantize(2)
+        banks = [product(2, 0, 2, 7), product(2, 2, 2, 0)]
+        weave(on_vector, 3, z, 2, 4)
+        quantize(3)
+        banks = banks + [product(3, 0, 2, 1), product(3, 2, 2, 2)]
+        leave(on_scalar, nc.sync, 2, 0, 2, banks[0])
+        leave(on_vector, nc.sync, 2, 2, 2, banks[1])
+        leave(on_scalar, nc.scalar, 3, 0, 2, banks[2])
+        leave(on_vector, nc.sync, 3, 2, 2, banks[3])

@@ -159,6 +159,13 @@ def tile_picked_ptrjump_none_p_kernel(tc, x_words, x_scales, w1, w2, offs, par, 
             engine_copy(res[:], bank[:])
             queue.dma_start(out_rows[:, u0 : u0 + rows, g * P : (g + 1) * P], res[:])
 
+        def keep_warm(g):
+            idle = psum.tile([P, N], F32, name="idle%d" % g, tag="bank%d" % (3 + g))
+            nc.tensor.matmul_mx(
+                out=idle[:], lhsT=z_codes[g][:].bitcast(FP8X4), lhsT_scale=z_sc[g][:],
+                rhs=w2_codes[:].bitcast(FP8X4), rhs_scale=w2_sc[:], start=True, stop=True,
+            )
+
         on_scalar, on_vector = nc.scalar.copy, nc.vector.tensor_copy
         z = second_hop(0)
         weave(on_scalar, 0, z, 0, 4)
@@ -167,11 +174,13 @@ def tile_picked_ptrjump_none_p_kernel(tc, x_words, x_scales, w1, w2, offs, par, 
         nc.vector.quantize_mx(out=w2_codes[:].bitcast(FP8X4), scales=w2_sc[:], in_=w2_bf[:].rearrange("p c j -> p (c j)"))
         quantize(0)
         bank = product(0, 0, 4, 5)
+        keep_warm(0)
         leave(on_scalar, nc.sync, 0, 0, 4, bank)
         z = second_hop(2)
         weave(on_scalar, 2, z, 0, 4)
         quantize(1)
         bank = product(1, 0, 4, 6)
+        keep_warm(1)
         z = second_hop(3)
         weave(on_scalar, 3, z, 0, 2)
         leave(on_scalar, nc.sync, 1, 0, 4, bank)

@@ -188,8 +188,10 @@ def tile_picked_ptrjump_none_p_kernel(tc, x_words, x_scales, w1, w2, offs, par, 
         banks = [product(2, 0, 2, 7), product(2, 2, 2, 0)]
         weave(on_vector, 3, z, 2, 4)
         quantize(3)
-        banks = banks + [product(3, 0, 2, 1), product(3, 2, 2, 2)]
+        banks = banks + [product(3, u, 1, 1 + u) for u in range(4)]
         leave(on_scalar, nc.sync, 2, 0, 2, banks[0])
         leave(on_vector, nc.sync, 2, 2, 2, banks[1])
-        leave(on_scalar, nc.scalar, 3, 0, 2, banks[2])
-        leave(on_vector, nc.sync, 3, 2, 2, banks[3])
+        leave(on_scalar, nc.sync, 3, 0, 1, banks[2])
+        leave(on_vector, nc.sync, 3, 1, 1, banks[3])
+        leave(on_scalar, nc.scalar, 3, 2, 1, banks[4])
+        leave(on_vector, nc.sync, 3, 3, 1, banks[5])

@@ -120,25 +120,26 @@ def tile_picked_ptrjump_none_p_kernel(tc, x_words, x_scales, w1, w2, offs, par, 
         w2_sc = keep.tile([P, N], U8, name="w2_sc", align_bytes=64)
 
         out_rows = out.rearrange("(u p) n -> p u n", p=P)
-        z_bf = [keep.tile([P, P, PACK], BF16, name="z_bf%d" % g, align_bytes=64) for g in range(PIECES)]
-        z_codes = [keep.tile([P, P], U32, name="z_codes%d" % g, align_bytes=64) for g in range(PIECES)]
-        z_sc = [keep.tile([P, P], U8, name="z_sc%d" % g, align_bytes=64) for g in range(PIECES)]
+        z_bf, z_codes, z_sc = {}, {}, {}
 
-        def second_hop(g):
-            z = keep.tile([P, PACK, P], F32, name="z%d" % g, tag="ring%d" % (g % 2), align_bytes=64)
-            for t in range(PACK):
+        def second_hop(g, z, lo, hi):
+            for t in range(lo, hi):
                 nc.vector.tensor_tensor(
-                    z[:, t, :], diff[t][:].indirect(par_t[:, g * 8 : (g + 1) * 8]), y_neg[t][:, g * P : (g + 1) * P], SUB
+                    z[:, (t - lo) * P : (t - lo + 1) * P], diff[t][:].indirect(par_t[:, g * 8 : (g + 1) * 8]),
+                    y_neg[t][:, g * P : (g + 1) * P], SUB,
                 )
-            return z
 
-        def weave(engine_copy, g, z, lo, hi):
+        def weave(engine_copy, g, z, lo, hi, tag):
+            if g not in z_bf:
+                z_bf[g] = keep.tile([P, P, PACK], BF16, name="z_bf%d" % g, tag=tag, align_bytes=64)
             engine_copy(
                 z_bf[g][:, :, lo:hi].rearrange("p (c i) t -> p c t i", i=4),
-                z[:, lo:hi, :].rearrange("p t (c i) -> p c t i", i=4),
+                z.rearrange("p (t c i) -> p c t i", c=P // 4, i=4),
             )
 
         def quantize(g):
+            z_codes[g] = keep.tile([P, P], U32, name="z_codes%d" % g, tag="z_codes%d" % g, align_bytes=64)
+            z_sc[g] = keep.tile([P, P], U8, name="z_sc%d" % g, tag="z_sc%d" % g, align_bytes=64)
             nc.vector.quantize_mx(
                 out=z_codes[g][:].bitcast(FP8X4), scales=z_sc[g][:], in_=z_bf[g][:].rearrange("p c t -> p (c t)")
             )
@@ -154,44 +155,58 @@ def tile_picked_ptrjump_none_p_kernel(tc, x_words, x_scales, w1, w2, offs, par, 
                 )
             return bank
 
-        def leave(engine_copy, queue, g, u0, rows, bank):
-            res = keep.tile([P, rows, P], F32, name="res%d_%d" % (g, u0))
-            engine_copy(res[:], bank[:])
-            queue.dma_start(out_rows[:, u0 : u0 + rows, g * P : (g + 1) * P], res[:])
+        def leave(engine_copy, g, u0, rows, bank):
+            engine_copy(res[g][:, u0 : u0 + rows, :], bank[:])
 
-        def keep_warm(g):
-            idle = psum.tile([P, N], F32, name="idle%d" % g, tag="bank%d" % (3 + g))
+        def store(g, queue, u0, rows):
+            queue.dma_start(out_rows[:, u0 : u0 + rows, g * P : (g + 1) * P], res[g][:, u0 : u0 + rows, :])
+
+        def keep_warm(bank_no):
+            idle = psum.tile([P, N], F32, name="idle%d" % bank_no, tag="bank%d" % bank_no)
             nc.tensor.matmul_mx(
-                out=idle[:], lhsT=z_codes[g][:].bitcast(FP8X4), lhsT_scale=z_sc[g][:],
+                out=idle[:], lhsT=z_codes[0][:].bitcast(FP8X4), lhsT_scale=z_sc[0][:],
                 rhs=w2_codes[:].bitcast(FP8X4), rhs_scale=w2_sc[:], start=True, stop=True,
             )
 
+        res = [keep.tile([P, PACK, P], F32, name="res%d" % g, align_bytes=64) for g in range(PIECES)]
         on_scalar, on_vector = nc.scalar.copy, nc.vector.tensor_copy
-        z = second_hop(0)
-        weave(on_scalar, 0, z, 0, 4)
-        z = second_hop(1)
-        weave(on_scalar, 1, z, 0, 4)
+        sums = keep.tile([P, 2 * S], F32, name="sums", tag="ring0", align_bytes=64)
+        for g in range(2):
+            second_hop(g, sums[:, g * S : (g + 1) * S], 0, 4)
+            weave(on_scalar, g, sums[:, g * S : (g + 1) * S], 0, 4, "z_bf%d" % g)
         nc.vector.quantize_mx(out=w2_codes[:].bitcast(FP8X4), scales=w2_sc[:], in_=w2_bf[:].rearrange("p c j -> p (c j)"))
         quantize(0)
-        bank = product(0, 0, 4, 5)
-        keep_warm(0)
-        leave(on_scalar, nc.sync, 0, 0, 4, bank)
-        z = second_hop(2)
-        weave(on_scalar, 2, z, 0, 4)
+        banks0 = [product(0, 0, 2, 5), product(0, 2, 2, 6)]
+        z2 = sums[:, S - P : 2 * S - P]
+        second_hop(2, z2[:, :P], 0, 1)
         quantize(1)
-        bank = product(1, 0, 4, 6)
-        keep_warm(1)
-        z = second_hop(3)
-        weave(on_scalar, 3, z, 0, 2)
-        leave(on_scalar, nc.sync, 1, 0, 4, bank)
+        banks1 = [product(1, 0, 2, 7), product(1, 2, 2, 0)]
+        leave(on_scalar, 0, 0, 2, banks0[0])
+        leave(on_scalar, 0, 2, 2, banks0[1])
+        store(0, nc.sync, 0, 4)
+        leave(on_scalar, 1, 0, 2, banks1[0])
+        keep_warm(6)
+        keep_warm(7)
+        second_hop(2, z2[:, P:], 1, 4)
+        weave(on_scalar, 2, z2, 0, 4, "z_codes1")
+        leave(on_scalar, 1, 2, 2, banks1[1])
+        store(1, nc.sync, 0, 4)
+        z3 = keep.tile([P, PACK * P], F32, name="z3", tag="z_bf1", align_bytes=64)
+        second_hop(3, z3[:], 0, 4)
+        weave(on_scalar, 3, z3[:, : 2 * P], 0, 2, "ring0")
         quantize(2)
-        banks = [product(2, 0, 2, 7), product(2, 2, 2, 0)]
-        weave(on_vector, 3, z, 2, 4)
+        banks2 = [product(2, 0, 1, 1), product(2, 1, 1, 2), product(2, 2, 2, 5)]
+        weave(on_vector, 3, z3[:, 2 * P :], 2, 4, "ring0")
         quantize(3)
-        banks = banks + [product(3, u, 1, 1 + u) for u in range(4)]
-        leave(on_scalar, nc.sync, 2, 0, 2, banks[0])
-        leave(on_vector, nc.sync, 2, 2, 2, banks[1])
-        leave(on_scalar, nc.sync, 3, 0, 1, banks[2])
-        leave(on_vector, nc.sync, 3, 1, 1, banks[3])
-        leave(on_scalar, nc.scalar, 3, 2, 1, banks[4])
-        leave(on_vector, nc.sync, 3, 3, 1, banks[5])
+        banks3 = [product(3, u, 1, (3, 4, 0, 6)[u]) for u in range(4)]
+        leave(on_scalar, 2, 0, 1, banks2[0])
+        leave(on_scalar, 2, 1, 1, banks2[1])
+        store(2, nc.sync, 0, 2)
+        leave(on_vector, 2, 2, 2, banks2[2])
+        store(2, nc.sync, 2, 2)
+        leave(on_vector, 3, 0, 1, banks3[0])
+        leave(on_scalar, 3, 1, 1, banks3[1])
+        store(3, nc.sync, 0, 2)
+        leave(on_vector, 3, 2, 1, banks3[2])
+        leave(on_scalar, 3, 3, 1, banks3[3])
+        store(3, nc.scalar, 2, 2)

@@ -122,11 +122,12 @@ def tile_picked_ptrjump_none_p_kernel(tc, x_words, x_scales, w1, w2, offs, par, 
         out_rows = out.rearrange("(u p) n -> p u n", p=P)
         z_bf, z_codes, z_sc = {}, {}, {}
 
-        def second_hop(g, z, lo, hi):
+        def second_hop(g, z, lo, hi, width=P):
             for t in range(lo, hi):
                 nc.vector.tensor_tensor(
-                    z[:, (t - lo) * P : (t - lo + 1) * P], diff[t][:].indirect(par_t[:, g * 8 : (g + 1) * 8]),
-                    y_neg[t][:, g * P : (g + 1) * P], SUB,
+                    z[:, (t - lo) * width : (t - lo + 1) * width],
+                    diff[t][:].indirect(par_t[:, g * 8 : g * 8 + width // 16]),
+                    y_neg[t][:, g * P : g * P + width], SUB,
                 )
 
         def weave(engine_copy, g, z, lo, hi, tag):
@@ -134,7 +135,7 @@ def tile_picked_ptrjump_none_p_kernel(tc, x_words, x_scales, w1, w2, offs, par, 
                 z_bf[g] = keep.tile([P, P, PACK], BF16, name="z_bf%d" % g, tag=tag, align_bytes=64)
             engine_copy(
                 z_bf[g][:, :, lo:hi].rearrange("p (c i) t -> p c t i", i=4),
-                z.rearrange("p (t c i) -> p c t i", c=P // 4, i=4),
+                z.rearrange("p t (c i) -> p c t i", i=4),
             )
 
         def quantize(g):
@@ -164,39 +165,40 @@ def tile_picked_ptrjump_none_p_kernel(tc, x_words, x_scales, w1, w2, offs, par, 
         def keep_warm(bank_no):
             idle = psum.tile([P, N], F32, name="idle%d" % bank_no, tag="bank%d" % bank_no)
             nc.tensor.matmul_mx(
-                out=idle[:], lhsT=z_codes[0][:].bitcast(FP8X4), lhsT_scale=z_sc[0][:],
+                out=idle[:], lhsT=z_codes[1][:].bitcast(FP8X4), lhsT_scale=z_sc[1][:],
                 rhs=w2_codes[:].bitcast(FP8X4), rhs_scale=w2_sc[:], start=True, stop=True,
             )
 
         res = [keep.tile([P, PACK, P], F32, name="res%d" % g, align_bytes=64) for g in range(PIECES)]
         on_scalar, on_vector = nc.scalar.copy, nc.vector.tensor_copy
-        sums = keep.tile([P, 2 * S], F32, name="sums", tag="ring0", align_bytes=64)
+        sums = keep.tile([P, 2 * S + HALF], F32, name="sums", tag="ring0", align_bytes=64)
+        second_hop(0, sums[:, HALF:], 0, 4, HALF)
+        z01 = sums[:, HALF:].rearrange("p (t n) -> p t n", t=PACK)
         for g in range(2):
-            second_hop(g, sums[:, g * S : (g + 1) * S], 0, 4)
-            weave(on_scalar, g, sums[:, g * S : (g + 1) * S], 0, 4, "z_bf%d" % g)
+            weave(on_scalar, g, z01[:, :, g * P : (g + 1) * P], 0, 4, "z_bf%d" % g)
         nc.vector.quantize_mx(out=w2_codes[:].bitcast(FP8X4), scales=w2_sc[:], in_=w2_bf[:].rearrange("p c j -> p (c j)"))
+        second_hop(2, sums[:, :HALF], 0, 2)
         quantize(0)
         banks0 = [product(0, 0, 2, 5), product(0, 2, 2, 6)]
-        z2 = sums[:, S - P : 2 * S - P]
-        second_hop(2, z2[:, :P], 0, 1)
+        second_hop(2, sums[:, 2 * P : 3 * P], 2, 3)
         quantize(1)
         banks1 = [product(1, 0, 2, 7), product(1, 2, 2, 0)]
+        second_hop(2, sums[:, 3 * P : S], 3, 4)
         leave(on_scalar, 0, 0, 2, banks0[0])
         leave(on_scalar, 0, 2, 2, banks0[1])
         store(0, nc.sync, 0, 4)
-        leave(on_scalar, 1, 0, 2, banks1[0])
+        keep_warm(5)
         keep_warm(6)
-        keep_warm(7)
-        second_hop(2, z2[:, P:], 1, 4)
-        weave(on_scalar, 2, z2, 0, 4, "z_codes1")
+        weave(on_scalar, 2, sums[:, :S].rearrange("p (t n) -> p t n", t=PACK), 0, 4, "z_codes0")
+        leave(on_scalar, 1, 0, 2, banks1[0])
+        z3 = keep.tile([P, PACK, P], F32, name="z3", tag="z_bf1", align_bytes=64)
+        second_hop(3, z3[:].rearrange("p t n -> p (t n)"), 0, 4)
+        weave(on_scalar, 3, z3[:, :2, :], 0, 2, "ring0")
         leave(on_scalar, 1, 2, 2, banks1[1])
         store(1, nc.sync, 0, 4)
-        z3 = keep.tile([P, PACK * P], F32, name="z3", tag="z_bf1", align_bytes=64)
-        second_hop(3, z3[:], 0, 4)
-        weave(on_scalar, 3, z3[:, : 2 * P], 0, 2, "ring0")
         quantize(2)
         banks2 = [product(2, 0, 1, 1), product(2, 1, 1, 2), product(2, 2, 2, 5)]
-        weave(on_vector, 3, z3[:, 2 * P :], 2, 4, "ring0")
+        weave(on_vector, 3, z3[:, 2:, :], 2, 4, "ring0")
         quantize(3)
         banks3 = [product(3, u, 1, (3, 4, 0, 6)[u]) for u in range(4)]
         leave(on_scalar, 2, 0, 1, banks2[0])

@@ -162,13 +162,6 @@ def tile_picked_ptrjump_none_p_kernel(tc, x_words, x_scales, w1, w2, offs, par, 
         def store(g, queue, u0, rows):
             queue.dma_start(out_rows[:, u0 : u0 + rows, g * P : (g + 1) * P], res[g][:, u0 : u0 + rows, :])
 
-        def keep_warm(bank_no):
-            idle = psum.tile([P, N], F32, name="idle%d" % bank_no, tag="bank%d" % bank_no)
-            nc.tensor.matmul_mx(
-                out=idle[:], lhsT=z_codes[1][:].bitcast(FP8X4), lhsT_scale=z_sc[1][:],
-                rhs=w2_codes[:].bitcast(FP8X4), rhs_scale=w2_sc[:], start=True, stop=True,
-            )
-
         res = [keep.tile([P, PACK, P], F32, name="res%d" % g, align_bytes=64) for g in range(PIECES)]
         on_scalar, on_vector = nc.scalar.copy, nc.vector.tensor_copy
         sums = keep.tile([P, 2 * S + HALF], F32, name="sums", tag="ring0", align_bytes=64)
@@ -187,8 +180,6 @@ def tile_picked_ptrjump_none_p_kernel(tc, x_words, x_scales, w1, w2, offs, par, 
         leave(on_scalar, 0, 0, 2, banks0[0])
         leave(on_scalar, 0, 2, 2, banks0[1])
         store(0, nc.sync, 0, 4)
-        keep_warm(5)
-        keep_warm(6)
         weave(on_scalar, 2, sums[:, :S].rearrange("p (t n) -> p t n", t=PACK), 0, 4, "z_codes0")
         leave(on_scalar, 1, 0, 2, banks1[0])
         z3 = keep.tile([P, PACK, P], F32, name="z3", tag="z_bf1", align_bytes=64)

@@ -75,14 +75,11 @@ def tile_picked_ptrjump_none_p_kernel(tc, x_words, x_scales, w1, w2, offs, par, 
                 out=w1_codes[t][:].bitcast(FP8X4), scales=w1_sc[t][:], in_=w1_bf[t][:].rearrange("p m j -> p (m j)")
             )
 
-        window = [
-            keep.tile([P, 2 * S if t in (1, 2) else S], F32, name="window%d" % t, align_bytes=64) for t in range(PACK)
-        ]
+        window = [keep.tile([P, S], F32, name="window%d" % t, align_bytes=64) for t in range(PACK)]
         y_last = [keep.tile([P, HALF], F32, name="y_last%d" % b, tag="ring%d" % b, align_bytes=64) for b in range(2)]
-        y2 = keep.tile([P, S], F32, name="y2")
         halves = [slice(0, HALF), slice(HALF, S)]
-        y_neg = [window[t][:, :S] for t in range(PACK)]
-        y_pos = [window[1][:, S:], window[2][:, S:], y2[:]]
+        y_neg = [window[t][:] for t in range(PACK)]
+        y_pos = [keep.tile([P, S], F32, name="y_pos%d" % t, align_bytes=64) for t in range(PACK - 1)]
         diff = [keep.tile([P, S], F32, name="diff%d" % t) for t in range(PACK)]
         for t in range(PACK):
             spans = halves if t == 0 else [slice(0, S)]
@@ -101,12 +98,9 @@ def tile_picked_ptrjump_none_p_kernel(tc, x_words, x_scales, w1, w2, offs, par, 
                 nc.vector.tensor_copy(y_pos[t][:, spans[1]], banks[1][:])
             else:
                 nc.scalar.activation(y_neg[t], banks[0][:], COPY, scale=-1.0)
-                if t < 3:
-                    nc.scalar.copy(y_pos[t], banks[0][:])
-                else:
-                    for b in range(2):
-                        nc.scalar.copy(y_last[b][:], banks[0][:, halves[b]])
-            for b, span in enumerate([slice(0, S)] if t in (1, 2) else halves):
+                for b, span in enumerate(halves):
+                    nc.scalar.copy(y_pos[t][:, span] if t < 3 else y_last[b][:], banks[0][:, span])
+            for b, span in enumerate(halves):
                 nc.vector.tensor_tensor(
                     diff[t][:, span], window[t][:].indirect(par_t[:, span.start // 16 : span.stop // 16]),
                     y_pos[t][:, span] if t < 3 else y_last[b][:], ADD,

@@ -158,23 +158,30 @@ def tile_picked_ptrjump_none_p_kernel(tc, x_words, x_scales, w1, w2, offs, par, 
 
         res = [keep.tile([P, PACK, P], F32, name="res%d" % g, align_bytes=64) for g in range(PIECES)]
         on_scalar, on_vector = nc.scalar.copy, nc.vector.tensor_copy
-        sums = keep.tile([P, 2 * S + HALF], F32, name="sums", tag="ring0", align_bytes=64)
-        second_hop(0, sums[:, HALF:], 0, 4, HALF)
-        z01 = sums[:, HALF:].rearrange("p (t n) -> p t n", t=PACK)
-        for g in range(2):
-            weave(on_scalar, g, z01[:, :, g * P : (g + 1) * P], 0, 4, "z_bf%d" % g)
+        sums = keep.tile([P, 2 * S], F32, name="sums", tag="ring0", align_bytes=64)
+        second_hop(0, sums[:], 0, 4, HALF)
+        z01 = sums[:].rearrange("p (t n) -> p t n", t=PACK)
+        z2 = sums[:, HALF:].rearrange("p (h k n) -> p h k n", h=2, k=3)[:, :, 0:3:2, :]
+        for lo in (0, 2):
+            for g in range(2):
+                weave(on_scalar, g, z01[:, lo : lo + 2, g * P : (g + 1) * P], lo, lo + 2, "z_bf%d" % g)
         nc.vector.quantize_mx(out=w2_codes[:].bitcast(FP8X4), scales=w2_sc[:], in_=w2_bf[:].rearrange("p c j -> p (c j)"))
-        second_hop(2, sums[:, :HALF], 0, 2)
+        second_hop(2, z2[:, 0, 0, :], 0, 1)
         quantize(0)
         banks0 = [product(0, 0, 2, 5), product(0, 2, 2, 6)]
-        second_hop(2, sums[:, 2 * P : 3 * P], 2, 3)
+        second_hop(2, z2[:, 0, 1, :], 1, 2)
         quantize(1)
         banks1 = [product(1, 0, 2, 7), product(1, 2, 2, 0)]
-        second_hop(2, sums[:, 3 * P : S], 3, 4)
+        second_hop(2, z2[:, 1, 0, :], 2, 3)
+        second_hop(2, z2[:, 1, 1, :], 3, 4)
         leave(on_scalar, 0, 0, 2, banks0[0])
         leave(on_scalar, 0, 2, 2, banks0[1])
         store(0, nc.sync, 0, 4)
-        weave(on_scalar, 2, sums[:, :S].rearrange("p (t n) -> p t n", t=PACK), 0, 4, "z_codes0")
+        z_bf[2] = keep.tile([P, P, PACK], BF16, name="z_bf2", tag="z_codes0", align_bytes=64)
+        nc.scalar.copy(
+            z_bf[2][:].rearrange("p (c i) (h u) -> p c h u i", i=4, h=2),
+            z2.rearrange("p h u (c i) -> p c h u i", i=4),
+        )
         leave(on_scalar, 1, 0, 2, banks1[0])
         z3 = keep.tile([P, PACK, P], F32, name="z3", tag="z_bf1", align_bytes=64)
         second_hop(3, z3[:].rearrange("p t n -> p (t n)"), 0, 4)

@@ -13,7 +13,6 @@ U16 = mybir.dt.uint16
 U8 = mybir.dt.uint8
 FP8X4 = mybir.dt.float8_e4m3fn_x4
 COPY = mybir.ActivationFunctionType.Copy
-ADD = mybir.AluOpType.add
 SUB = mybir.AluOpType.subtract
 
 P = 128
@@ -76,65 +75,81 @@ def tile_picked_ptrjump_none_p_kernel(tc, x_words, x_scales, w1, w2, offs, par, 
             )
 
         window = [keep.tile([P, S], F32, name="window%d" % t, align_bytes=64) for t in range(PACK)]
-        y_last = [keep.tile([P, HALF], F32, name="y_last%d" % b, tag="ring%d" % b, align_bytes=64) for b in range(2)]
+        hop = [keep.tile([P, S], F32, name="hop%d" % t, align_bytes=64) for t in range(PACK)]
+        base = keep.tile([P, 2, PACK, HALF], F32, name="base", align_bytes=64)
+        drop = keep.tile([P, 2, PACK, HALF], F32, name="drop", align_bytes=64)
         halves = [slice(0, HALF), slice(HALF, S)]
-        y_neg = [window[t][:] for t in range(PACK)]
-        y_pos = [keep.tile([P, S], F32, name="y_pos%d" % t, align_bytes=64) for t in range(PACK - 1)]
-        diff = [keep.tile([P, S], F32, name="diff%d" % t) for t in range(PACK)]
-        for t in range(PACK):
-            spans = halves if t == 0 else [slice(0, S)]
-            banks = []
-            for b, span in enumerate(spans):
-                bank = psum.tile([P, span.stop - span.start], F32, name="y_bank%d_%d" % (t, b), tag="bank%d" % (t + b + min(t, 1)))
-                nc.tensor.matmul_mx(
-                    out=bank[:], lhsT=w1_codes[t][:].bitcast(FP8X4), lhsT_scale=w1_sc[t][:],
-                    rhs=x_codes[:, span].bitcast(FP8X4), rhs_scale=x_sc[:, span], start=True, stop=True,
-                )
-                banks.append(bank)
-            if t == 0:
-                nc.scalar.activation(y_neg[t][:, spans[0]], banks[0][:], COPY, scale=-1.0)
-                nc.vector.tensor_scalar_mul(y_neg[t][:, spans[1]], banks[1][:], -1.0)
-                nc.scalar.copy(y_pos[t][:, spans[0]], banks[0][:])
-                nc.vector.tensor_copy(y_pos[t][:, spans[1]], banks[1][:])
-            else:
-                nc.scalar.activation(y_neg[t], banks[0][:], COPY, scale=-1.0)
-                for b, span in enumerate(halves):
-                    nc.scalar.copy(y_pos[t][:, span] if t < 3 else y_last[b][:], banks[0][:, span])
-            for b, span in enumerate(halves):
-                nc.vector.tensor_tensor(
-                    diff[t][:, span], window[t][:].indirect(par_t[:, span.start // 16 : span.stop // 16]),
-                    y_pos[t][:, span] if t < 3 else y_last[b][:], ADD,
-                )
 
-        w2_bf = keep.tile([P, N, PACK], BF16, name="w2_bf", tag="w1_codes3", align_bytes=64)
-        nc.scalar.copy(
-            w2_bf[:].rearrange("p (c i) j -> p c j i", i=4), w2_raw[:].rearrange("p j (c i) -> p c j i", i=4)
-        )
+        def looked_up(tile, h):
+            return tile[:].indirect(par_t[:, h * HALF // 16 : (h + 1) * HALF // 16])
+
+        def first_product(t, span, bank_no):
+            bank = psum.tile([P, span.stop - span.start], F32, name="y_bank%d" % bank_no, tag="bank%d" % bank_no)
+            nc.tensor.matmul_mx(
+                out=bank[:], lhsT=w1_codes[t][:].bitcast(FP8X4), lhsT_scale=w1_sc[t][:],
+                rhs=x_codes[:, span].bitcast(FP8X4), rhs_scale=x_sc[:, span], start=True, stop=True,
+            )
+            return bank
+
+        banks = [first_product(0, halves[h], h) for h in range(2)]
+        y_bank = [None] + [first_product(t, slice(0, S), t + 1) for t in range(1, PACK)]
+        nc.scalar.copy(window[0][:, halves[0]], banks[0][:])
+        nc.vector.tensor_copy(window[0][:, halves[1]], banks[1][:])
+        nc.scalar.copy(base[:, 0, 0, :], banks[0][:])
+        nc.vector.tensor_copy(base[:, 1, 0, :], banks[1][:])
+        nc.scalar.copy(window[1][:], y_bank[1][:])
+        for h in range(2):
+            nc.vector.tensor_tensor(hop[0][:, halves[h]], looked_up(window[0], h), base[:, h, 0, :], SUB)
+        nc.vector.tensor_copy(base[:, :, 1, :], window[1][:].rearrange("p (h n) -> p h n", h=2))
+        for h in range(2):
+            nc.vector.tensor_tensor(hop[1][:, halves[h]], looked_up(window[1], h), base[:, h, 1, :], SUB)
+        for t in (2, 3):
+            nc.scalar.copy(window[t][:], y_bank[t][:])
+            for h in range(2):
+                nc.scalar.activation(hop[t][:, halves[h]], looked_up(window[t], h), COPY)
+                if t == 3:
+                    nc.sync.dma_start(base[:, h, t, :], hop[t][:, halves[h]])
+            if t == 2:
+                nc.sync.dma_start(base[:, :, t, :], hop[t][:].rearrange("p (h n) -> p h n", h=2))
+
+        w2_bf = keep.tile([P, N, PACK], BF16, name="w2_bf", align_bytes=64)
         w2_codes = keep.tile([P, N], U32, name="w2_codes", align_bytes=64)
         w2_sc = keep.tile([P, N], U8, name="w2_sc", align_bytes=64)
 
-        out_rows = out.rearrange("(u p) n -> p u n", p=P)
-        z_bf, z_codes, z_sc = {}, {}, {}
-
-        def second_hop(g, z, lo, hi, width=P):
-            for t in range(lo, hi):
-                nc.vector.tensor_tensor(
-                    z[:, (t - lo) * width : (t - lo + 1) * width],
-                    diff[t][:].indirect(par_t[:, g * 8 : g * 8 + width // 16]),
-                    y_neg[t][:, g * P : g * P + width], SUB,
-                )
-
-        def weave(engine_copy, g, z, lo, hi, tag):
-            if g not in z_bf:
-                z_bf[g] = keep.tile([P, P, PACK], BF16, name="z_bf%d" % g, tag=tag, align_bytes=64)
+        def cast_w2(engine_copy, span):
             engine_copy(
-                z_bf[g][:, :, lo:hi].rearrange("p (c i) t -> p c t i", i=4),
-                z.rearrange("p t (c i) -> p c t i", i=4),
+                w2_bf[:, span, :].rearrange("p (c i) j -> p c j i", i=4),
+                w2_raw[:, :, span].rearrange("p j (c i) -> p c j i", i=4),
+            )
+
+        on_scalar, on_vector = nc.scalar.copy, nc.vector.tensor_copy
+        for h in range(2):
+            nc.vector.tensor_tensor(drop[:, h, 2, :], looked_up(hop[2], h), window[2][:, halves[h]], SUB)
+        cast_w2(on_vector, halves[0])
+        cast_w2(on_scalar, halves[1])
+        for h in range(2):
+            nc.vector.tensor_tensor(drop[:, h, 3, :], looked_up(hop[3], h), window[3][:, halves[h]], SUB)
+        for h in range(2):
+            for t in range(2):
+                nc.scalar.activation(drop[:, h, t, :], looked_up(hop[t], h), COPY)
+        nc.vector.quantize_mx(out=w2_codes[:].bitcast(FP8X4), scales=w2_sc[:], in_=w2_bf[:].rearrange("p c j -> p (c j)"))
+
+        out_rows = out.rearrange("(u p) n -> p u n", p=P)
+        z_bf = [keep.tile([P, P, PACK], BF16, name="z_bf%d" % g, align_bytes=64) for g in range(PIECES)]
+        z_codes = [keep.tile([P, P], U32, name="z_codes%d" % g, align_bytes=64) for g in range(PIECES)]
+        z_sc = [keep.tile([P, P], U8, name="z_sc%d" % g, align_bytes=64) for g in range(PIECES)]
+        res = [keep.tile([P, PACK, P], F32, name="res%d" % g, align_bytes=64) for g in range(PIECES)]
+
+        def weave(g):
+            cols = slice(g % 2 * P, (g % 2 + 1) * P)
+            nc.vector.tensor_tensor(
+                z_bf[g][:].rearrange("p (c i) t -> p c t i", i=4),
+                base[:, g // 2, :, cols].rearrange("p t (c i) -> p c t i", i=4),
+                drop[:, g // 2, :, cols].rearrange("p t (c i) -> p c t i", i=4),
+                SUB,
             )
 
         def quantize(g):
-            z_codes[g] = keep.tile([P, P], U32, name="z_codes%d" % g, tag="z_codes%d" % g, align_bytes=64)
-            z_sc[g] = keep.tile([P, P], U8, name="z_sc%d" % g, tag="z_sc%d" % g, align_bytes=64)
             nc.vector.quantize_mx(
                 out=z_codes[g][:].bitcast(FP8X4), scales=z_sc[g][:], in_=z_bf[g][:].rearrange("p c t -> p (c t)")
             )
@@ -156,47 +171,23 @@ def tile_picked_ptrjump_none_p_kernel(tc, x_words, x_scales, w1, w2, offs, par, 
         def store(g, queue, u0, rows):
             queue.dma_start(out_rows[:, u0 : u0 + rows, g * P : (g + 1) * P], res[g][:, u0 : u0 + rows, :])
 
-        res = [keep.tile([P, PACK, P], F32, name="res%d" % g, align_bytes=64) for g in range(PIECES)]
-        on_scalar, on_vector = nc.scalar.copy, nc.vector.tensor_copy
-        sums = keep.tile([P, 2 * S], F32, name="sums", tag="ring0", align_bytes=64)
-        second_hop(0, sums[:], 0, 4, HALF)
-        z01 = sums[:].rearrange("p (t n) -> p t n", t=PACK)
-        z2 = sums[:, HALF:].rearrange("p (h k n) -> p h k n", h=2, k=3)[:, :, 0:3:2, :]
-        for lo in (0, 2):
-            for g in range(2):
-                weave(on_scalar, g, z01[:, lo : lo + 2, g * P : (g + 1) * P], lo, lo + 2, "z_bf%d" % g)
-        nc.vector.quantize_mx(out=w2_codes[:].bitcast(FP8X4), scales=w2_sc[:], in_=w2_bf[:].rearrange("p c j -> p (c j)"))
-        second_hop(2, z2[:, 0, 0, :], 0, 1)
+        weave(0)
+        weave(1)
         quantize(0)
-        banks0 = [product(0, 0, 2, 5), product(0, 2, 2, 6)]
-        second_hop(2, z2[:, 0, 1, :], 1, 2)
-        quantize(1)
-        banks1 = [product(1, 0, 2, 7), product(1, 2, 2, 0)]
-        second_hop(2, z2[:, 1, 0, :], 2, 3)
-        second_hop(2, z2[:, 1, 1, :], 3, 4)
-        leave(on_scalar, 0, 0, 2, banks0[0])
-        leave(on_scalar, 0, 2, 2, banks0[1])
+        leave(on_scalar, 0, 0, 4, product(0, 0, 4, 5))
         store(0, nc.sync, 0, 4)
-        z_bf[2] = keep.tile([P, P, PACK], BF16, name="z_bf2", tag="z_codes0", align_bytes=64)
-        nc.scalar.copy(
-            z_bf[2][:].rearrange("p (c i) (h u) -> p c h u i", i=4, h=2),
-            z2.rearrange("p h u (c i) -> p c h u i", i=4),
-        )
-        leave(on_scalar, 1, 0, 2, banks1[0])
-        z3 = keep.tile([P, PACK, P], F32, name="z3", tag="z_bf1", align_bytes=64)
-        second_hop(3, z3[:].rearrange("p t n -> p (t n)"), 0, 4)
-        weave(on_scalar, 3, z3[:, :2, :], 0, 2, "ring0")
-        leave(on_scalar, 1, 2, 2, banks1[1])
+        weave(2)
+        quantize(1)
+        leave(on_scalar, 1, 0, 4, product(1, 0, 4, 6))
         store(1, nc.sync, 0, 4)
+        weave(3)
         quantize(2)
-        banks2 = [product(2, 0, 1, 1), product(2, 1, 1, 2), product(2, 2, 2, 5)]
-        weave(on_vector, 3, z3[:, 2:, :], 2, 4, "ring0")
+        banks2 = [product(2, 0, 2, 7), product(2, 2, 2, 0)]
         quantize(3)
-        banks3 = [product(3, u, 1, (3, 4, 0, 6)[u]) for u in range(4)]
-        leave(on_scalar, 2, 0, 1, banks2[0])
-        leave(on_scalar, 2, 1, 1, banks2[1])
+        banks3 = [product(3, u, 1, u + 1) for u in range(4)]
+        leave(on_scalar, 2, 0, 2, banks2[0])
         store(2, nc.sync, 0, 2)
-        leave(on_vector, 2, 2, 2, banks2[2])
+        leave(on_vector, 2, 2, 2, banks2[1])
         store(2, nc.sync, 2, 2)
         leave(on_vector, 3, 0, 1, banks3[0])
         leave(on_scalar, 3, 1, 1, banks3[1])

@@ -18,7 +18,6 @@ SUB = mybir.AluOpType.subtract
 P = 128
 PACK = 4
 HALF = S // 2
-PIECES = 4
 X_FIRST = 1024
 
 
@@ -112,40 +111,48 @@ def tile_picked_ptrjump_none_p_kernel(tc, x_words, x_scales, w1, w2, offs, par, 
             if t == 2:
                 nc.sync.dma_start(base[:, :, t, :], hop[t][:].rearrange("p (h n) -> p h n", h=2))
 
-        w2_bf = keep.tile([P, N, PACK], BF16, name="w2_bf", align_bytes=64)
-        w2_codes = keep.tile([P, N], U32, name="w2_codes", align_bytes=64)
-        w2_sc = keep.tile([P, N], U8, name="w2_sc", align_bytes=64)
+        w2_bf = [keep.tile([P, HALF, PACK], BF16, name="w2_bf%d" % h, align_bytes=64) for h in range(2)]
+        w2_codes = [keep.tile([P, HALF], U32, name="w2_codes%d" % h, align_bytes=64) for h in range(2)]
+        w2_sc = {}
+        on_scalar, on_vector = nc.scalar.copy, nc.vector.tensor_copy
 
-        def cast_w2(engine_copy, span):
+        def cast_w2(engine_copy, h):
             engine_copy(
-                w2_bf[:, span, :].rearrange("p (c i) j -> p c j i", i=4),
-                w2_raw[:, :, span].rearrange("p j (c i) -> p c j i", i=4),
+                w2_bf[h][:].rearrange("p (c i) j -> p c j i", i=4),
+                w2_raw[:, :, halves[h]].rearrange("p j (c i) -> p c j i", i=4),
             )
 
-        on_scalar, on_vector = nc.scalar.copy, nc.vector.tensor_copy
-        for h in range(2):
-            nc.vector.tensor_tensor(drop[:, h, 2, :], looked_up(hop[2], h), window[2][:, halves[h]], SUB)
-        cast_w2(on_vector, halves[0])
-        cast_w2(on_scalar, halves[1])
-        for h in range(2):
-            nc.vector.tensor_tensor(drop[:, h, 3, :], looked_up(hop[3], h), window[3][:, halves[h]], SUB)
-        for h in range(2):
-            for t in range(2):
-                nc.scalar.activation(drop[:, h, t, :], looked_up(hop[t], h), COPY)
-        nc.vector.quantize_mx(out=w2_codes[:].bitcast(FP8X4), scales=w2_sc[:], in_=w2_bf[:].rearrange("p c j -> p (c j)"))
+        def quantize_w2(h, tag):
+            w2_sc[h] = keep.tile([P, HALF], U8, name="w2_sc%d" % h, tag=tag, align_bytes=64)
+            nc.vector.quantize_mx(
+                out=w2_codes[h][:].bitcast(FP8X4), scales=w2_sc[h][:], in_=w2_bf[h][:].rearrange("p c j -> p (c j)")
+            )
+
+        def second_hop(t, lo, hi):
+            h = lo // HALF
+            picked = hop[t][:].indirect(par_t[:, lo // 16 : hi // 16])
+            dst = drop[:, h, t, lo - h * HALF : hi - h * HALF]
+            if t < 2:
+                nc.scalar.activation(dst, picked, COPY)
+            else:
+                nc.vector.tensor_tensor(dst, picked, window[t][:, lo:hi], SUB)
 
         out_rows = out.rearrange("(u p) n -> p u n", p=P)
-        z_bf = [keep.tile([P, P, PACK], BF16, name="z_bf%d" % g, align_bytes=64) for g in range(PIECES)]
-        z_codes = [keep.tile([P, P], U32, name="z_codes%d" % g, align_bytes=64) for g in range(PIECES)]
-        z_sc = [keep.tile([P, P], U8, name="z_sc%d" % g, align_bytes=64) for g in range(PIECES)]
-        res = [keep.tile([P, PACK, P], F32, name="res%d" % g, align_bytes=64) for g in range(PIECES)]
+        pieces = [(g * P, (g + 1) * P) for g in range(S // P)]
+        widths = [hi - lo for lo, hi in pieces]
+        z_bf = [keep.tile([P, w, PACK], BF16, name="z_bf%d" % g, tag="z_bf%d" % g, align_bytes=64) for g, w in enumerate(widths)]
+        z_codes = [keep.tile([P, w], U32, name="z_codes%d" % g, align_bytes=64) for g, w in enumerate(widths)]
+        z_sc = [keep.tile([P, w], U8, name="z_sc%d" % g, align_bytes=64) for g, w in enumerate(widths)]
+        res = [keep.tile([P, PACK, w], F32, name="res%d" % g, align_bytes=64) for g, w in enumerate(widths)]
 
         def weave(g):
-            cols = slice(g % 2 * P, (g % 2 + 1) * P)
+            lo, hi = pieces[g]
+            h = lo // HALF
+            cols = slice(lo - h * HALF, hi - h * HALF)
             nc.vector.tensor_tensor(
                 z_bf[g][:].rearrange("p (c i) t -> p c t i", i=4),
-                base[:, g // 2, :, cols].rearrange("p t (c i) -> p c t i", i=4),
-                drop[:, g // 2, :, cols].rearrange("p t (c i) -> p c t i", i=4),
+                base[:, h, :, cols].rearrange("p t (c i) -> p c t i", i=4),
+                drop[:, h, :, cols].rearrange("p t (c i) -> p c t i", i=4),
                 SUB,
             )
 
@@ -155,12 +162,12 @@ def tile_picked_ptrjump_none_p_kernel(tc, x_words, x_scales, w1, w2, offs, par, 
             )
 
         def product(g, u0, rows, bank_no):
-            bank = psum.tile([P, rows, P], F32, name="o_bank%d_%d" % (g, u0), tag="bank%d" % bank_no)
+            bank = psum.tile([P, rows, widths[g]], F32, name="o_bank%d_%d" % (g, u0), tag="bank%d" % bank_no)
             for v in range(rows):
                 u = u0 + v
+                cols = slice(u % 2 * P, (u % 2 + 1) * P)
                 nc.tensor.matmul_mx(
-                    out=bank[:, v, :], lhsT=w2_codes[:, u * P : (u + 1) * P].bitcast(FP8X4),
-                    lhsT_scale=w2_sc[:, u * P : (u + 1) * P],
+                    out=bank[:, v, :], lhsT=w2_codes[u // 2][:, cols].bitcast(FP8X4), lhsT_scale=w2_sc[u // 2][:, cols],
                     rhs=z_codes[g][:].bitcast(FP8X4), rhs_scale=z_sc[g][:], start=True, stop=True,
                 )
             return bank
@@ -169,25 +176,41 @@ def tile_picked_ptrjump_none_p_kernel(tc, x_words, x_scales, w1, w2, offs, par, 
             engine_copy(res[g][:, u0 : u0 + rows, :], bank[:])
 
         def store(g, queue, u0, rows):
-            queue.dma_start(out_rows[:, u0 : u0 + rows, g * P : (g + 1) * P], res[g][:, u0 : u0 + rows, :])
+            lo, hi = pieces[g]
+            queue.dma_start(out_rows[:, u0 : u0 + rows, lo:hi], res[g][:, u0 : u0 + rows, :])
 
+        cast_w2(on_vector, 0)
+        second_hop(2, 0, HALF)
+        quantize_w2(0, "w2_sc0")
+        second_hop(2, HALF, S)
+        for h in range(2):
+            second_hop(3, h * HALF, (h + 1) * HALF)
+        for h in range(2):
+            for t in range(2):
+                second_hop(t, h * HALF, (h + 1) * HALF)
+        cast_w2(on_scalar, 1)
         weave(0)
         weave(1)
         quantize(0)
-        leave(on_scalar, 0, 0, 4, product(0, 0, 4, 5))
-        store(0, nc.sync, 0, 4)
+        leave(on_scalar, 0, 0, 2, product(0, 0, 2, 5))
+        store(0, nc.sync, 0, 2)
         weave(2)
         quantize(1)
-        leave(on_scalar, 1, 0, 4, product(1, 0, 4, 6))
-        store(1, nc.sync, 0, 4)
-        weave(3)
+        leave(on_scalar, 1, 0, 2, product(1, 0, 2, 6))
+        store(1, nc.sync, 0, 2)
+        quantize_w2(1, "z_bf0")
+        late = [product(0, 2, 2, 7), product(1, 2, 2, 0)]
+        for g in range(2):
+            leave(on_scalar, g, 2, 2, late[g])
+            store(g, nc.sync, 2, 2)
         quantize(2)
-        banks2 = [product(2, 0, 2, 7), product(2, 2, 2, 0)]
+        banks2 = [product(2, 0, 2, 5), product(2, 2, 2, 6)]
+        weave(3)
         quantize(3)
         banks3 = [product(3, u, 1, u + 1) for u in range(4)]
         leave(on_scalar, 2, 0, 2, banks2[0])
         store(2, nc.sync, 0, 2)
-        leave(on_vector, 2, 2, 2, banks2[1])
+        leave(on_scalar, 2, 2, 2, banks2[1])
         store(2, nc.sync, 2, 2)
         leave(on_vector, 3, 0, 1, banks3[0])
         leave(on_scalar, 3, 1, 1, banks3[1])

@@ -75,8 +75,10 @@ def tile_picked_ptrjump_none_p_kernel(tc, x_words, x_scales, w1, w2, offs, par, 
 
         window = [keep.tile([P, S], F32, name="window%d" % t, align_bytes=64) for t in range(PACK)]
         hop = [keep.tile([P, S], F32, name="hop%d" % t, align_bytes=64) for t in range(PACK)]
-        base = keep.tile([P, 2, PACK, HALF], F32, name="base", align_bytes=64)
-        drop = keep.tile([P, 2, PACK, HALF], F32, name="drop", align_bytes=64)
+        planes = keep.tile([P, (3 * PACK - 1) * HALF], F32, name="planes", align_bytes=64)
+        base = planes[:, (PACK - 1) * HALF :].rearrange("p (h t n) -> p h t n", h=2, t=PACK)
+        drop_first = keep.tile([P, PACK, HALF], F32, name="drop_first", tag="drop_first", align_bytes=64)
+        drop = [drop_first[:], planes[:, : PACK * HALF].rearrange("p (t n) -> p t n", t=PACK)]
         halves = [slice(0, HALF), slice(HALF, S)]
 
         def looked_up(tile, h):
@@ -131,90 +133,82 @@ def tile_picked_ptrjump_none_p_kernel(tc, x_words, x_scales, w1, w2, offs, par, 
         def second_hop(t, lo, hi):
             h = lo // HALF
             picked = hop[t][:].indirect(par_t[:, lo // 16 : hi // 16])
-            dst = drop[:, h, t, lo - h * HALF : hi - h * HALF]
+            dst = drop[h][:, t, lo - h * HALF : hi - h * HALF]
             if t < 2:
                 nc.scalar.activation(dst, picked, COPY)
             else:
                 nc.vector.tensor_tensor(dst, picked, window[t][:, lo:hi], SUB)
 
         out_rows = out.rearrange("(u p) n -> p u n", p=P)
-        pieces = [(g * P, (g + 1) * P) for g in range(S // P)]
-        widths = [hi - lo for lo, hi in pieces]
-        z_bf = [keep.tile([P, w, PACK], BF16, name="z_bf%d" % g, tag="z_bf%d" % g, align_bytes=64) for g, w in enumerate(widths)]
-        z_codes = [keep.tile([P, w], U32, name="z_codes%d" % g, align_bytes=64) for g, w in enumerate(widths)]
-        z_sc = [keep.tile([P, w], U8, name="z_sc%d" % g, align_bytes=64) for g, w in enumerate(widths)]
-        res = [keep.tile([P, PACK, w], F32, name="res%d" % g, align_bytes=64) for g, w in enumerate(widths)]
+        z_bf = keep.tile([P, S * PACK], BF16, name="z_bf", align_bytes=64)
+        z_codes = keep.tile([P, S], U32, name="z_codes", align_bytes=64)
+        z_sc = keep.tile([P, S], U8, name="z_sc", align_bytes=64)
+        res = keep.tile([P, PACK, S], F32, name="res", align_bytes=64)
 
-        def weave(g):
-            lo, hi = pieces[g]
+        def weave(lo, hi):
             h = lo // HALF
             cols = slice(lo - h * HALF, hi - h * HALF)
             nc.vector.tensor_tensor(
-                z_bf[g][:].rearrange("p (c i) t -> p c t i", i=4),
+                z_bf[:, lo * PACK : hi * PACK].rearrange("p (c i t) -> p c t i", i=4, t=PACK),
                 base[:, h, :, cols].rearrange("p t (c i) -> p c t i", i=4),
-                drop[:, h, :, cols].rearrange("p t (c i) -> p c t i", i=4),
+                drop[h][:, :, cols].rearrange("p t (c i) -> p c t i", i=4),
                 SUB,
             )
 
-        def quantize(g):
+        def quantize(lo, hi):
             nc.vector.quantize_mx(
-                out=z_codes[g][:].bitcast(FP8X4), scales=z_sc[g][:], in_=z_bf[g][:].rearrange("p c t -> p (c t)")
+                out=z_codes[:, lo:hi].bitcast(FP8X4), scales=z_sc[:, lo:hi], in_=z_bf[:, lo * PACK : hi * PACK]
             )
 
-        def product(g, u0, rows, bank_no):
-            bank = psum.tile([P, rows, widths[g]], F32, name="o_bank%d_%d" % (g, u0), tag="bank%d" % bank_no)
+        def product(lo, hi, u0, rows, bank_no):
+            bank = psum.tile([P, rows, hi - lo], F32, name="o_bank%d_%d" % (lo, u0), tag="bank%d" % bank_no)
             for v in range(rows):
                 u = u0 + v
                 cols = slice(u % 2 * P, (u % 2 + 1) * P)
                 nc.tensor.matmul_mx(
                     out=bank[:, v, :], lhsT=w2_codes[u // 2][:, cols].bitcast(FP8X4), lhsT_scale=w2_sc[u // 2][:, cols],
-                    rhs=z_codes[g][:].bitcast(FP8X4), rhs_scale=z_sc[g][:], start=True, stop=True,
+                    rhs=z_codes[:, lo:hi].bitcast(FP8X4), rhs_scale=z_sc[:, lo:hi], start=True, stop=True,
                 )
-            return bank
+            return bank, res[:, u0 : u0 + rows, lo:hi]
 
-        def leave(engine_copy, g, u0, rows, bank):
-            engine_copy(res[g][:, u0 : u0 + rows, :], bank[:])
+        def leave(engine_copy, made):
+            engine_copy(made[1], made[0][:])
 
-        def store(g, queue, u0, rows):
-            lo, hi = pieces[g]
-            queue.dma_start(out_rows[:, u0 : u0 + rows, lo:hi], res[g][:, u0 : u0 + rows, :])
+        def store(queue, lo, hi, u0, rows):
+            queue.dma_start(out_rows[:, u0 : u0 + rows, lo:hi], res[:, u0 : u0 + rows, lo:hi])
 
+        third, fourth = (HALF, 3 * P), (3 * P, S)
         cast_w2(on_vector, 0)
         second_hop(2, 0, HALF)
         quantize_w2(0, "w2_sc0")
+        second_hop(3, 0, HALF)
         second_hop(2, HALF, S)
-        for h in range(2):
-            second_hop(3, h * HALF, (h + 1) * HALF)
-        for h in range(2):
-            for t in range(2):
-                second_hop(t, h * HALF, (h + 1) * HALF)
+        second_hop(0, 0, HALF)
+        second_hop(1, 0, HALF)
         cast_w2(on_scalar, 1)
-        weave(0)
-        weave(1)
-        quantize(0)
-        leave(on_scalar, 0, 0, 2, product(0, 0, 2, 5))
-        store(0, nc.sync, 0, 2)
-        weave(2)
-        quantize(1)
-        leave(on_scalar, 1, 0, 2, product(1, 0, 2, 6))
-        store(1, nc.sync, 0, 2)
-        quantize_w2(1, "z_bf0")
-        late = [product(0, 2, 2, 7), product(1, 2, 2, 0)]
-        for g in range(2):
-            leave(on_scalar, g, 2, 2, late[g])
-            store(g, nc.sync, 2, 2)
-        quantize(2)
-        banks2 = [product(2, 0, 2, 5), product(2, 2, 2, 6)]
-        weave(3)
-        quantize(3)
-        banks3 = [product(3, u, 1, u + 1) for u in range(4)]
-        leave(on_scalar, 2, 0, 2, banks2[0])
-        store(2, nc.sync, 0, 2)
-        leave(on_scalar, 2, 2, 2, banks2[1])
-        store(2, nc.sync, 2, 2)
-        leave(on_vector, 3, 0, 1, banks3[0])
-        leave(on_scalar, 3, 1, 1, banks3[1])
-        store(3, nc.sync, 0, 2)
-        leave(on_vector, 3, 2, 1, banks3[2])
-        leave(on_scalar, 3, 3, 1, banks3[3])
-        store(3, nc.scalar, 2, 2)
+        second_hop(0, HALF, S)
+        second_hop(1, *third)
+        second_hop(1, *fourth)
+        weave(0, P)
+        weave(P, HALF)
+        second_hop(3, *third)
+        quantize(0, HALF)
+        quantize_w2(1, "drop_first")
+        for u in range(PACK):
+            leave(on_scalar, product(0, HALF, u, 1, (5 + u) % 8))
+            store(nc.sync, 0, HALF, u, 1)
+        weave(*third)
+        second_hop(3, *fourth)
+        quantize(*third)
+        for u0 in (0, 2):
+            leave(on_scalar, product(*third, u0, 2, 1 + u0 // 2))
+            store(nc.sync, *third, u0, 2)
+        weave(*fourth)
+        quantize(*fourth)
+        last = [product(*fourth, u, 1, 3 + u) for u in range(PACK)]
+        leave(on_vector, last[0])
+        leave(on_scalar, last[1])
+        store(nc.sync, *fourth, 0, 2)
+        leave(on_vector, last[2])
+        leave(on_scalar, last[3])
+        store(nc.scalar, *fourth, 2, 2)

@@ -104,14 +104,14 @@ def tile_picked_ptrjump_none_p_kernel(tc, x_words, x_scales, w1, w2, offs, par, 
         nc.vector.tensor_copy(base[:, :, 1, :], window[1][:].rearrange("p (h n) -> p h n", h=2))
         for h in range(2):
             nc.vector.tensor_tensor(hop[1][:, halves[h]], looked_up(window[1], h), base[:, h, 1, :], SUB)
-        for t in (2, 3):
-            nc.scalar.copy(window[t][:], y_bank[t][:])
-            for h in range(2):
-                nc.scalar.activation(hop[t][:, halves[h]], looked_up(window[t], h), COPY)
-                if t == 3:
-                    nc.sync.dma_start(base[:, h, t, :], hop[t][:, halves[h]])
-            if t == 2:
-                nc.sync.dma_start(base[:, :, t, :], hop[t][:].rearrange("p (h n) -> p h n", h=2))
+        nc.scalar.copy(window[2][:], y_bank[2][:])
+        nc.scalar.copy(window[3][:], y_bank[3][:])
+        for h in range(2):
+            nc.scalar.activation(hop[2][:, halves[h]], looked_up(window[2], h), COPY)
+        nc.sync.dma_start(base[:, :, 2, :], hop[2][:].rearrange("p (h n) -> p h n", h=2))
+        for lo, hi in ((0, P), (P, HALF), (HALF, S)):
+            nc.scalar.activation(hop[3][:, lo:hi], window[3][:].indirect(par_t[:, lo // 16 : hi // 16]), COPY)
+            nc.sync.dma_start(base[:, lo // HALF, 3, lo % HALF : lo % HALF + hi - lo], hop[3][:, lo:hi])
 
         w2_bf = [keep.tile([P, HALF, PACK], BF16, name="w2_bf%d" % h, align_bytes=64) for h in range(2)]
         w2_codes = [keep.tile([P, HALF], U32, name="w2_codes%d" % h, align_bytes=64) for h in range(2)]
@@ -183,12 +183,13 @@ def tile_picked_ptrjump_none_p_kernel(tc, x_words, x_scales, w1, w2, offs, par, 
         quantize_w2(0, "w2_sc0")
         second_hop(3, 0, HALF)
         second_hop(2, HALF, S)
-        second_hop(0, 0, HALF)
-        second_hop(1, 0, HALF)
+        for lo in (0, P):
+            for t in range(2):
+                second_hop(t, lo, lo + P)
         cast_w2(on_scalar, 1)
-        second_hop(0, HALF, S)
-        second_hop(1, *third)
-        second_hop(1, *fourth)
+        for piece in (third, fourth):
+            for t in range(2):
+                second_hop(t, *piece)
         weave(0, P)
         weave(P, HALF)
         second_hop(3, *third)

@@ -99,9 +99,9 @@ def tile_picked_ptrjump_none_p_kernel(tc, x_words, x_scales, w1, w2, offs, par, 
         nc.scalar.copy(base[:, 0, 0, :], banks[0][:])
         nc.vector.tensor_copy(base[:, 1, 0, :], banks[1][:])
         nc.scalar.copy(window[1][:], y_bank[1][:])
-        for h in range(2):
-            nc.vector.tensor_tensor(hop[0][:, halves[h]], looked_up(window[0], h), base[:, h, 0, :], SUB)
+        nc.vector.tensor_tensor(hop[0][:, halves[0]], looked_up(window[0], 0), base[:, 0, 0, :], SUB)
         nc.vector.tensor_copy(base[:, :, 1, :], window[1][:].rearrange("p (h n) -> p h n", h=2))
+        nc.vector.tensor_tensor(hop[0][:, halves[1]], looked_up(window[0], 1), base[:, 1, 0, :], SUB)
         for h in range(2):
             nc.vector.tensor_tensor(hop[1][:, halves[h]], looked_up(window[1], h), base[:, h, 1, :], SUB)
         nc.scalar.copy(window[2][:], y_bank[2][:])
@@ -183,9 +183,8 @@ def tile_picked_ptrjump_none_p_kernel(tc, x_words, x_scales, w1, w2, offs, par, 
         quantize_w2(0, "w2_sc0")
         second_hop(3, 0, HALF)
         second_hop(2, HALF, S)
-        for lo in (0, P):
-            for t in range(2):
-                second_hop(t, lo, lo + P)
+        second_hop(0, 0, HALF)
+        second_hop(1, 0, HALF)
         cast_w2(on_scalar, 1)
         for piece in (third, fourth):
             for t in range(2):

@@ -31,7 +31,9 @@ def tile_picked_ptrjump_none_p_kernel(tc, x_words, x_scales, w1, w2, offs, par, 
         par_t = keep.tile([P, S // 16], U16, name="par_t")
         words = keep.tile([P, T], U32, name="words", tag="words", align_bytes=64)
         scale_rows = keep.tile([P, T], U8, name="scale_rows", align_bytes=64)
-        w1_raw = [keep.tile([P, PACK // 2, H], F32, name="w1_raw%d" % h) for h in range(2)]
+        wide = keep.tile([P, S + 2 * H], F32, name="wide", align_bytes=64)
+        w1_last = keep.tile([P, PACK // 2, H], F32, name="w1_last")
+        w1_raw = [wide[:, S:].rearrange("p (j c) -> p j c", j=2), w1_last[:]]
 
         nc.vector.memset(scale_rows[:].bitcast(I32), 0)
         x_rows = x_words[0].rearrange("p n r -> p (n r)").bitcast(I32)
@@ -42,7 +44,7 @@ def tile_picked_ptrjump_none_p_kernel(tc, x_words, x_scales, w1, w2, offs, par, 
         nc.sync.dma_start(words[:, X_FIRST:].bitcast(I32), x_rows[:, X_FIRST:])
         w1_rows = w1.rearrange("(p j) c -> p j c", j=PACK)
         for h in range(2):
-            nc.sync.dma_start(w1_raw[h][:], w1_rows[:, 2 * h : 2 * h + 2, :])
+            nc.sync.dma_start(w1_raw[h], w1_rows[:, 2 * h : 2 * h + 2, :])
 
         x_codes = keep.tile([P, S], U32, name="x_codes", align_bytes=64)
         x_sc = keep.tile([P, S], U8, name="x_sc", align_bytes=64)
@@ -61,7 +63,7 @@ def tile_picked_ptrjump_none_p_kernel(tc, x_words, x_scales, w1, w2, offs, par, 
         w1_sc = [keep.tile([P, P], U8, name="w1_sc%d" % t, align_bytes=64) for t in range(PACK)]
         w1_bf = [keep.tile([P, P, PACK], BF16, name="w1_bf%d" % t, align_bytes=64) for t in range(PACK)]
         for h in range(2):
-            src = w1_raw[h][:].rearrange("p j (b t r) -> p t b r j", t=PACK, r=8)
+            src = w1_raw[h].rearrange("p j (b t r) -> p t b r j", t=PACK, r=8)
             for t in range(PACK):
                 dst = w1_bf[t][:, :, 2 * h : 2 * h + 2].rearrange("p (b r) j -> p b r j", r=8)
                 if t < 2:
@@ -73,7 +75,7 @@ def tile_picked_ptrjump_none_p_kernel(tc, x_words, x_scales, w1, w2, offs, par, 
                 out=w1_codes[t][:].bitcast(FP8X4), scales=w1_sc[t][:], in_=w1_bf[t][:].rearrange("p m j -> p (m j)")
             )
 
-        window = [keep.tile([P, S], F32, name="window%d" % t, align_bytes=64) for t in range(PACK)]
+        window = [wide if t == 2 else keep.tile([P, S], F32, name="window%d" % t, align_bytes=64) for t in range(PACK)]
         hop = [keep.tile([P, S], F32, name="hop%d" % t, align_bytes=64) for t in range(PACK)]
         planes = keep.tile([P, (3 * PACK - 1) * HALF], F32, name="planes", align_bytes=64)
         base = planes[:, (PACK - 1) * HALF :].rearrange("p (h t n) -> p h t n", h=2, t=PACK)
@@ -104,10 +106,9 @@ def tile_picked_ptrjump_none_p_kernel(tc, x_words, x_scales, w1, w2, offs, par, 
         nc.vector.tensor_tensor(hop[0][:, halves[1]], looked_up(window[0], 1), base[:, 1, 0, :], SUB)
         for h in range(2):
             nc.vector.tensor_tensor(hop[1][:, halves[h]], looked_up(window[1], h), base[:, h, 1, :], SUB)
-        nc.scalar.copy(window[2][:], y_bank[2][:])
+        nc.scalar.copy(window[2][:, :S], y_bank[2][:])
         nc.scalar.copy(window[3][:], y_bank[3][:])
-        for h in range(2):
-            nc.scalar.activation(hop[2][:, halves[h]], looked_up(window[2], h), COPY)
+        nc.scalar.activation(hop[2][:], window[2][:].indirect(par_t[:]), COPY)
         nc.sync.dma_start(base[:, :, 2, :], hop[2][:].rearrange("p (h n) -> p h n", h=2))
         for lo, hi in ((0, P), (P, HALF), (HALF, S)):
             nc.scalar.activation(hop[3][:, lo:hi], window[3][:].indirect(par_t[:, lo // 16 : hi // 16]), COPY)

@@ -27,12 +27,12 @@ def tile_picked_ptrjump_none_p_kernel(tc, x_words, x_scales, w1, w2, offs, par, 
         keep = ctx.enter_context(tc.tile_pool(name="keep", bufs=1))
         psum = ctx.enter_context(tc.psum_pool(name="psum", bufs=1))
 
-        offs_t = keep.tile([P, S // 16], U16, name="offs_t")
-        par_t = keep.tile([P, S // 16], U16, name="par_t")
-        words = keep.tile([P, T], U32, name="words", tag="words", align_bytes=64)
-        scale_rows = keep.tile([P, T], U8, name="scale_rows", align_bytes=64)
-        wide = keep.tile([P, S + 2 * H], F32, name="wide", align_bytes=64)
-        w1_last = keep.tile([P, PACK // 2, H], F32, name="w1_last")
+        offs_t = keep.tile([P, S // 16], U16, name="offs_t", align_bytes=256)
+        par_t = keep.tile([P, S // 16], U16, name="par_t", align_bytes=256)
+        words = keep.tile([P, T], U32, name="words", tag="words", align_bytes=256)
+        scale_rows = keep.tile([P, T], U8, name="scale_rows", align_bytes=256)
+        wide = keep.tile([P, S + 2 * H], F32, name="wide", align_bytes=256)
+        w1_last = keep.tile([P, PACK // 2, H], F32, name="w1_last", align_bytes=256)
         w1_raw = [wide[:, S:].rearrange("p (j c) -> p j c", j=2), w1_last[:]]
 
         nc.vector.memset(scale_rows[:].bitcast(I32), 0)
@@ -46,22 +46,22 @@ def tile_picked_ptrjump_none_p_kernel(tc, x_words, x_scales, w1, w2, offs, par, 
         for h in range(2):
             nc.sync.dma_start(w1_raw[h], w1_rows[:, 2 * h : 2 * h + 2, :])
 
-        x_codes = keep.tile([P, S], U32, name="x_codes", align_bytes=64)
-        x_sc = keep.tile([P, S], U8, name="x_sc", align_bytes=64)
-        picked_rows = keep.tile([P, S], U8, name="picked_rows", align_bytes=64)
+        x_codes = keep.tile([P, S], U32, name="x_codes", align_bytes=256)
+        x_sc = keep.tile([P, S], U8, name="x_sc", align_bytes=256)
+        picked_rows = keep.tile([P, S], U8, name="picked_rows", align_bytes=256)
         nc.vector.memset(x_sc[:].bitcast(I32), 0)
         nc.vector.tensor_copy(picked_rows[:], scale_rows[:].indirect(offs_t[:]))
         for r in range(4):
             nc.sync.dma_start(x_sc[r:P:32, :].bitcast(I32), picked_rows[8 * r : P : 32, :].bitcast(I32))
         nc.vector.tensor_copy(x_codes[:], words[:].indirect(offs_t[:]))
-        w2_raw = keep.tile([P, PACK, N], F32, name="w2_raw", tag="words", align_bytes=64)
+        w2_raw = keep.tile([P, PACK, N], F32, name="w2_raw", tag="words", align_bytes=256)
         w2_rows = w2.rearrange("(b t r) c -> t b r c", t=PACK, r=8)
         for t in range(PACK):
             nc.sync.dma_start(w2_raw[:, t, :], w2_rows[t])
 
-        w1_codes = [keep.tile([P, P], U32, name="w1_codes%d" % t, tag="w1_codes%d" % t, align_bytes=64) for t in range(PACK)]
-        w1_sc = [keep.tile([P, P], U8, name="w1_sc%d" % t, align_bytes=64) for t in range(PACK)]
-        w1_bf = [keep.tile([P, P, PACK], BF16, name="w1_bf%d" % t, align_bytes=64) for t in range(PACK)]
+        w1_codes = [keep.tile([P, P], U32, name="w1_codes%d" % t, tag="w1_codes%d" % t, align_bytes=256) for t in range(PACK)]
+        w1_sc = [keep.tile([P, P], U8, name="w1_sc%d" % t, align_bytes=256) for t in range(PACK)]
+        w1_bf = [keep.tile([P, P, PACK], BF16, name="w1_bf%d" % t, align_bytes=256) for t in range(PACK)]
         for h in range(2):
             src = w1_raw[h].rearrange("p j (b t r) -> p t b r j", t=PACK, r=8)
             for t in range(PACK):
@@ -75,11 +75,11 @@ def tile_picked_ptrjump_none_p_kernel(tc, x_words, x_scales, w1, w2, offs, par, 
                 out=w1_codes[t][:].bitcast(FP8X4), scales=w1_sc[t][:], in_=w1_bf[t][:].rearrange("p m j -> p (m j)")
             )
 
-        window = [wide if t == 2 else keep.tile([P, S], F32, name="window%d" % t, align_bytes=64) for t in range(PACK)]
-        hop = [keep.tile([P, S], F32, name="hop%d" % t, align_bytes=64) for t in range(PACK)]
-        planes = keep.tile([P, (3 * PACK - 1) * HALF], F32, name="planes", align_bytes=64)
+        window = [wide if t == 2 else keep.tile([P, S], F32, name="window%d" % t, align_bytes=256) for t in range(PACK)]
+        hop = [keep.tile([P, S], F32, name="hop%d" % t, align_bytes=256) for t in range(PACK)]
+        planes = keep.tile([P, (3 * PACK - 1) * HALF], F32, name="planes", align_bytes=256)
         base = planes[:, (PACK - 1) * HALF :].rearrange("p (h t n) -> p h t n", h=2, t=PACK)
-        drop_first = keep.tile([P, PACK, HALF], F32, name="drop_first", tag="drop_first", align_bytes=64)
+        drop_first = keep.tile([P, PACK, HALF], F32, name="drop_first", tag="drop_first", align_bytes=256)
         drop = [drop_first[:], planes[:, : PACK * HALF].rearrange("p (t n) -> p t n", t=PACK)]
         halves = [slice(0, HALF), slice(HALF, S)]
 
@@ -114,8 +114,8 @@ def tile_picked_ptrjump_none_p_kernel(tc, x_words, x_scales, w1, w2, offs, par, 
             nc.scalar.activation(hop[3][:, lo:hi], window[3][:].indirect(par_t[:, lo // 16 : hi // 16]), COPY)
             nc.sync.dma_start(base[:, lo // HALF, 3, lo % HALF : lo % HALF + hi - lo], hop[3][:, lo:hi])
 
-        w2_bf = [keep.tile([P, HALF, PACK], BF16, name="w2_bf%d" % h, align_bytes=64) for h in range(2)]
-        w2_codes = [keep.tile([P, HALF], U32, name="w2_codes%d" % h, align_bytes=64) for h in range(2)]
+        w2_bf = [keep.tile([P, HALF, PACK], BF16, name="w2_bf%d" % h, align_bytes=256) for h in range(2)]
+        w2_codes = [keep.tile([P, HALF], U32, name="w2_codes%d" % h, align_bytes=256) for h in range(2)]
         w2_sc = {}
         on_scalar, on_vector = nc.scalar.copy, nc.vector.tensor_copy
 
@@ -126,7 +126,7 @@ def tile_picked_ptrjump_none_p_kernel(tc, x_words, x_scales, w1, w2, offs, par, 
             )
 
         def quantize_w2(h, tag):
-            w2_sc[h] = keep.tile([P, HALF], U8, name="w2_sc%d" % h, tag=tag, align_bytes=64)
+            w2_sc[h] = keep.tile([P, HALF], U8, name="w2_sc%d" % h, tag=tag, align_bytes=256)
             nc.vector.quantize_mx(
                 out=w2_codes[h][:].bitcast(FP8X4), scales=w2_sc[h][:], in_=w2_bf[h][:].rearrange("p c j -> p (c j)")
             )
@@ -141,10 +141,10 @@ def tile_picked_ptrjump_none_p_kernel(tc, x_words, x_scales, w1, w2, offs, par, 
                 nc.vector.tensor_tensor(dst, picked, window[t][:, lo:hi], SUB)
 
         out_rows = out.rearrange("(u p) n -> p u n", p=P)
-        z_bf = keep.tile([P, S * PACK], BF16, name="z_bf", align_bytes=64)
-        z_codes = keep.tile([P, S], U32, name="z_codes", align_bytes=64)
-        z_sc = keep.tile([P, S], U8, name="z_sc", align_bytes=64)
-        res = keep.tile([P, PACK, S], F32, name="res", align_bytes=64)
+        z_bf = keep.tile([P, S * PACK], BF16, name="z_bf", align_bytes=256)
+        z_codes = keep.tile([P, S], U32, name="z_codes", align_bytes=256)
+        z_sc = keep.tile([P, S], U8, name="z_sc", align_bytes=256)
+        res = keep.tile([P, PACK, S], F32, name="res", align_bytes=256)
 
         def weave(lo, hi):
             h = lo // HALF

from contextlib import ExitStack

import concourse.mybir as mybir

K, T, S, H, N = 512, 2048, 512, 512, 512
FLOPS = 2 * K * H * S + 2 * H * N * S

F32 = mybir.dt.float32
BF16 = mybir.dt.bfloat16
I32 = mybir.dt.int32
U32 = mybir.dt.uint32
U16 = mybir.dt.uint16
U8 = mybir.dt.uint8
FP8X4 = mybir.dt.float8_e4m3fn_x4
COPY = mybir.ActivationFunctionType.Copy
SUB = mybir.AluOpType.subtract

P = 128
PACK = 4
HALF = S // 2
X_FIRST = 1024


def tile_picked_ptrjump_none_p_kernel(tc, x_words, x_scales, w1, w2, offs, par, out):
    nc = tc.nc
    with ExitStack() as ctx:
        keep = ctx.enter_context(tc.tile_pool(name="keep", bufs=1))
        psum = ctx.enter_context(tc.psum_pool(name="psum", bufs=1))

        offs_t = keep.tile([P, S // 16], U16, name="offs_t", align_bytes=256)
        par_t = keep.tile([P, S // 16], U16, name="par_t", align_bytes=256)
        words = keep.tile([P, T], U32, name="words", tag="words", align_bytes=256)
        scale_rows = keep.tile([P, T], U8, name="scale_rows", align_bytes=256)
        wide = keep.tile([P, S + 2 * H], F32, name="wide", align_bytes=256)
        w1_last = keep.tile([P, PACK // 2, H], F32, name="w1_last", align_bytes=256)
        w1_raw = [wide[:, S:].rearrange("p (j c) -> p j c", j=2), w1_last[:]]

        nc.vector.memset(scale_rows[:].bitcast(I32), 0)
        x_rows = x_words[0].rearrange("p n r -> p (n r)").bitcast(I32)
        nc.sync.dma_start(offs_t[:], offs)
        nc.scalar.dma_start(words[:, :X_FIRST].bitcast(I32), x_rows[:, :X_FIRST])
        nc.sync.dma_start(par_t[:], par)
        nc.sync.dma_start(scale_rows[0:P:8, :].bitcast(I32), x_scales[0].bitcast(I32))
        nc.sync.dma_start(words[:, X_FIRST:].bitcast(I32), x_rows[:, X_FIRST:])
        w1_rows = w1.rearrange("(p j) c -> p j c", j=PACK)
        for h in range(2):
            nc.sync.dma_start(w1_raw[h], w1_rows[:, 2 * h : 2 * h + 2, :])

        x_codes = keep.tile([P, S], U32, name="x_codes", align_bytes=256)
        x_sc = keep.tile([P, S], U8, name="x_sc", align_bytes=256)
        picked_rows = keep.tile([P, S], U8, name="picked_rows", align_bytes=256)
        nc.vector.memset(x_sc[:].bitcast(I32), 0)
        nc.vector.tensor_copy(picked_rows[:], scale_rows[:].indirect(offs_t[:]))
        for r in range(4):
            nc.sync.dma_start(x_sc[r:P:32, :].bitcast(I32), picked_rows[8 * r : P : 32, :].bitcast(I32))
        nc.vector.tensor_copy(x_codes[:], words[:].indirect(offs_t[:]))
        w2_raw = keep.tile([P, PACK, N], F32, name="w2_raw", tag="words", align_bytes=256)
        w2_rows = w2.rearrange("(b t r) c -> t b r c", t=PACK, r=8)
        for t in range(PACK):
            nc.sync.dma_start(w2_raw[:, t, :], w2_rows[t])

        w1_codes = [keep.tile([P, P], U32, name="w1_codes%d" % t, tag="w1_codes%d" % t, align_bytes=256) for t in range(PACK)]
        w1_sc = [keep.tile([P, P], U8, name="w1_sc%d" % t, align_bytes=256) for t in range(PACK)]
        w1_bf = [keep.tile([P, P, PACK], BF16, name="w1_bf%d" % t, align_bytes=256) for t in range(PACK)]
        for h in range(2):
            src = w1_raw[h].rearrange("p j (b t r) -> p t b r j", t=PACK, r=8)
            for t in range(PACK):
                dst = w1_bf[t][:, :, 2 * h : 2 * h + 2].rearrange("p (b r) j -> p b r j", r=8)
                if t < 2:
                    nc.vector.tensor_copy(dst, src[:, t])
                else:
                    nc.scalar.activation(dst, src[:, t], COPY)
        for t in range(PACK):
            nc.vector.quantize_mx(
                out=w1_codes[t][:].bitcast(FP8X4), scales=w1_sc[t][:], in_=w1_bf[t][:].rearrange("p m j -> p (m j)")
            )

        window = [wide if t == 2 else keep.tile([P, S], F32, name="window%d" % t, align_bytes=256) for t in range(PACK)]
        hop = [keep.tile([P, S], F32, name="hop%d" % t, align_bytes=256) for t in range(PACK)]
        planes = keep.tile([P, (3 * PACK - 1) * HALF], F32, name="planes", align_bytes=256)
        base = planes[:, (PACK - 1) * HALF :].rearrange("p (h t n) -> p h t n", h=2, t=PACK)
        drop_first = keep.tile([P, PACK, HALF], F32, name="drop_first", tag="drop_first", align_bytes=256)
        drop = [drop_first[:], planes[:, : PACK * HALF].rearrange("p (t n) -> p t n", t=PACK)]
        halves = [slice(0, HALF), slice(HALF, S)]

        def looked_up(tile, h):
            return tile[:].indirect(par_t[:, h * HALF // 16 : (h + 1) * HALF // 16])

        def first_product(t, span, bank_no):
            bank = psum.tile([P, span.stop - span.start], F32, name="y_bank%d" % bank_no, tag="bank%d" % bank_no)
            nc.tensor.matmul_mx(
                out=bank[:], lhsT=w1_codes[t][:].bitcast(FP8X4), lhsT_scale=w1_sc[t][:],
                rhs=x_codes[:, span].bitcast(FP8X4), rhs_scale=x_sc[:, span], start=True, stop=True,
            )
            return bank

        banks = [first_product(0, halves[h], h) for h in range(2)]
        y_bank = [None] + [first_product(t, slice(0, S), t + 1) for t in range(1, PACK)]
        nc.scalar.copy(window[0][:, halves[0]], banks[0][:])
        nc.vector.tensor_copy(window[0][:, halves[1]], banks[1][:])
        nc.scalar.copy(base[:, 0, 0, :], banks[0][:])
        nc.vector.tensor_copy(base[:, 1, 0, :], banks[1][:])
        nc.scalar.copy(window[1][:], y_bank[1][:])
        nc.vector.tensor_tensor(hop[0][:, halves[0]], looked_up(window[0], 0), base[:, 0, 0, :], SUB)
        nc.vector.tensor_copy(base[:, :, 1, :], window[1][:].rearrange("p (h n) -> p h n", h=2))
        nc.vector.tensor_tensor(hop[0][:, halves[1]], looked_up(window[0], 1), base[:, 1, 0, :], SUB)
        for h in range(2):
            nc.vector.tensor_tensor(hop[1][:, halves[h]], looked_up(window[1], h), base[:, h, 1, :], SUB)
        nc.scalar.copy(window[2][:, :S], y_bank[2][:])
        nc.scalar.copy(window[3][:], y_bank[3][:])
        nc.scalar.activation(hop[2][:], window[2][:].indirect(par_t[:]), COPY)
        nc.sync.dma_start(base[:, :, 2, :], hop[2][:].rearrange("p (h n) -> p h n", h=2))
        for lo, hi in ((0, P), (P, HALF), (HALF, S)):
            nc.scalar.activation(hop[3][:, lo:hi], window[3][:].indirect(par_t[:, lo // 16 : hi // 16]), COPY)
            nc.sync.dma_start(base[:, lo // HALF, 3, lo % HALF : lo % HALF + hi - lo], hop[3][:, lo:hi])

        w2_bf = [keep.tile([P, HALF, PACK], BF16, name="w2_bf%d" % h, align_bytes=256) for h in range(2)]
        w2_codes = [keep.tile([P, HALF], U32, name="w2_codes%d" % h, align_bytes=256) for h in range(2)]
        w2_sc = {}
        on_scalar, on_vector = nc.scalar.copy, nc.vector.tensor_copy

        def cast_w2(engine_copy, h):
            engine_copy(
                w2_bf[h][:].rearrange("p (c i) j -> p c j i", i=4),
                w2_raw[:, :, halves[h]].rearrange("p j (c i) -> p c j i", i=4),
            )

        def quantize_w2(h, tag):
            w2_sc[h] = keep.tile([P, HALF], U8, name="w2_sc%d" % h, tag=tag, align_bytes=256)
            nc.vector.quantize_mx(
                out=w2_codes[h][:].bitcast(FP8X4), scales=w2_sc[h][:], in_=w2_bf[h][:].rearrange("p c j -> p (c j)")
            )

        def second_hop(t, lo, hi):
            h = lo // HALF
            picked = hop[t][:].indirect(par_t[:, lo // 16 : hi // 16])
            dst = drop[h][:, t, lo - h * HALF : hi - h * HALF]
            if t < 2:
                nc.scalar.activation(dst, picked, COPY)
            else:
                nc.vector.tensor_tensor(dst, picked, window[t][:, lo:hi], SUB)

        out_rows = out.rearrange("(u p) n -> p u n", p=P)
        z_bf = keep.tile([P, S * PACK], BF16, name="z_bf", align_bytes=256)
        z_codes = keep.tile([P, S], U32, name="z_codes", align_bytes=256)
        z_sc = keep.tile([P, S], U8, name="z_sc", align_bytes=256)
        res = keep.tile([P, PACK, S], F32, name="res", align_bytes=256)

        def weave(lo, hi):
            h = lo // HALF
            cols = slice(lo - h * HALF, hi - h * HALF)
            nc.vector.tensor_tensor(
                z_bf[:, lo * PACK : hi * PACK].rearrange("p (c i t) -> p c t i", i=4, t=PACK),
                base[:, h, :, cols].rearrange("p t (c i) -> p c t i", i=4),
                drop[h][:, :, cols].rearrange("p t (c i) -> p c t i", i=4),
                SUB,
            )

        def quantize(lo, hi):
            nc.vector.quantize_mx(
                out=z_codes[:, lo:hi].bitcast(FP8X4), scales=z_sc[:, lo:hi], in_=z_bf[:, lo * PACK : hi * PACK]
            )

        def product(lo, hi, u0, rows, bank_no):
            bank = psum.tile([P, rows, hi - lo], F32, name="o_bank%d_%d" % (lo, u0), tag="bank%d" % bank_no)
            for v in range(rows):
                u = u0 + v
                cols = slice(u % 2 * P, (u % 2 + 1) * P)
                nc.tensor.matmul_mx(
                    out=bank[:, v, :], lhsT=w2_codes[u // 2][:, cols].bitcast(FP8X4), lhsT_scale=w2_sc[u // 2][:, cols],
                    rhs=z_codes[:, lo:hi].bitcast(FP8X4), rhs_scale=z_sc[:, lo:hi], start=True, stop=True,
                )
            return bank, res[:, u0 : u0 + rows, lo:hi]

        def leave(engine_copy, made):
            engine_copy(made[1], made[0][:])

        def store(queue, lo, hi, u0, rows):
            queue.dma_start(out_rows[:, u0 : u0 + rows, lo:hi], res[:, u0 : u0 + rows, lo:hi])

        third, fourth = (HALF, 3 * P), (3 * P, S)
        cast_w2(on_vector, 0)
        second_hop(2, 0, HALF)
        quantize_w2(0, "w2_sc0")
        second_hop(3, 0, HALF)
        second_hop(2, HALF, S)
        second_hop(0, 0, HALF)
        second_hop(1, 0, HALF)
        cast_w2(on_scalar, 1)
        for piece in (third, fourth):
            for t in range(2):
                second_hop(t, *piece)
        weave(0, P)
        weave(P, HALF)
        second_hop(3, *third)
        quantize(0, HALF)
        quantize_w2(1, "drop_first")
        for u in range(PACK):
            leave(on_scalar, product(0, HALF, u, 1, (5 + u) % 8))
            store(nc.sync, 0, HALF, u, 1)
        weave(*third)
        second_hop(3, *fourth)
        quantize(*third)
        for u0 in (0, 2):
            leave(on_scalar, product(*third, u0, 2, 1 + u0 // 2))
            store(nc.sync, *third, u0, 2)
        weave(*fourth)
        quantize(*fourth)
        last = [product(*fourth, u, 1, 3 + u) for u in range(PACK)]
        leave(on_vector, last[0])
        leave(on_scalar, last[1])
        store(nc.sync, *fourth, 0, 2)
        leave(on_vector, last[2])
        leave(on_scalar, last[3])
        store(nc.scalar, *fourth, 2, 2)
